import numpy as np
import ml_dtypes


def mxq(x, axis, fmt="e4m3"):
    dtype, down = {"e4m3": (ml_dtypes.float8_e4m3fn, 7), "e5m2": (ml_dtypes.float8_e5m2, 14)}[fmt]
    v = np.moveaxis(np.asarray(x, np.float32).astype(ml_dtypes.bfloat16).astype(np.float64), axis, -1)
    blocks = v.reshape(v.shape[:-1] + (-1, 32))
    amax = np.abs(blocks).max(-1, keepdims=True)
    byte = np.maximum(np.where(amax > 0, np.frexp(amax)[1] - 1 + 127, 0) - down, 1)
    scale = np.exp2(byte - 127.0)
    codes = (blocks / scale).astype(np.float32).astype(dtype).astype(np.float64)
    return np.moveaxis((codes * scale).reshape(v.shape), -1, axis)


WIDE = False


def mx_kscale(k):
    if not WIDE:
        return np.ones(k)
    levels = np.array([10, -10, 5, -5, 0])
    if k % 512:
        return np.exp2(np.random.permutation(np.resize(levels, k // 32))).repeat(32)
    a = np.empty((k // 512, 16))
    for p in range(k // 512):
        a[p, :8] = np.random.permutation(np.resize(levels, 8))
        for g in range(8):
            far = levels[np.abs(levels - a[p, g]) >= 10]
            a[p, g + 8] = far[np.random.randint(len(far))]
    return np.exp2(a.ravel()).repeat(32)


def f64(x):
    return np.asarray(x).astype(np.float64)


def striped(idx):
    return np.tile(idx.reshape(-1, 16).T, (8, 1)).astype(np.uint16)


def unstriped(offs):
    return offs[:16].T.reshape(-1).astype(np.int64)


def pack_weight(w):
    k, n = w.shape
    w = f64(np.asarray(w, np.float32).astype(ml_dtypes.bfloat16)).reshape(k // 32, 32, n)
    amax = np.abs(w).max(1)
    byte = np.clip(np.where(amax > 0, np.frexp(amax)[1] - 1 + 127 - 7, 1), 1, 254)
    scaled = (w * np.exp2(127.0 - byte)[:, None, :]).reshape(k, n).astype(np.float32)
    words = np.ascontiguousarray(scaled.reshape(k // 512, 128, 4, n).transpose(0, 1, 3, 2)).astype(ml_dtypes.float8_e4m3fn).view(np.uint8)
    return words, np.ascontiguousarray(byte.astype(np.uint8).reshape(k // 512, 16, n))


def unpack_weight(words, scales):
    g, p, n, _ = words.shape
    vals = np.ascontiguousarray(words).view(ml_dtypes.float8_e4m3fn).astype(np.float64) * np.repeat(np.exp2(scales.astype(np.float64) - 127.0), 8, axis=1)[..., None]
    return vals.transpose(0, 1, 3, 2).reshape(g * 512, n)


def gelu(v):
    return 0.5 * v * (1.0 + np.tanh(np.sqrt(2.0 / np.pi) * (v + 0.044715 * v**3)))


K, T, S, N, U = 512, 2048, 1024, 128, 2048


def setup_inputs():
    n = np.random.standard_normal
    s = mx_kscale(K)[:, None]
    packed_w1 = pack_weight(n((K, N)) / np.sqrt(K) / s)
    return {
        "xT": (n((K, T)) * s).astype(np.float32),
        "w1_words": packed_w1[0],
        "w1_scales": packed_w1[1],
        "res": n((N, U)).astype(np.float32),
        "offs": striped(np.random.permutation(T)[:S]),
        "own": striped(np.random.randint(0, S, U)),
    }


def reference(xT, w1_words, w1_scales, res, offs, own):
    xq = mxq(f64(xT)[:, unstriped(offs)], 0, "e4m3")
    y = gelu(unpack_weight(w1_words, w1_scales).T @ xq)
    return f64(res) + y[:, unstriped(own)]

@@ -1,0 +1,125 @@
+from contextlib import ExitStack
+
+import concourse.mybir as mybir
+
+K, T, S, N, U = 512, 2048, 1024, 128, 2048
+FLOPS = 2 * K * N * S
+
+F32 = mybir.dt.float32
+BF16 = mybir.dt.bfloat16
+I32 = mybir.dt.int32
+U32 = mybir.dt.uint32
+U16 = mybir.dt.uint16
+U8 = mybir.dt.uint8
+FP8X4 = mybir.dt.float8_e4m3fn_x4
+GELU = mybir.ActivationFunctionType.Gelu_apprx_tanh
+COPY = mybir.ActivationFunctionType.Copy
+ADD = mybir.AluOpType.add
+
+P = 128
+PACK = 4
+LIST_COL = 16
+
+CHUNKS = ((1024, 1024), (1024, 512, 256, 256))
+PIECE = 256
+OUT_PIECES = (512, 512, 512, 256, 128, 128)
+
+
+def tile_picked_unmerge_gelu_e_kernel(tc, xT, w1_words, w1_scales, res, offs, own, out):
+    nc = tc.nc
+    with ExitStack() as ctx:
+        keep = ctx.enter_context(tc.tile_pool(name="keep", bufs=1))
+        psum = ctx.enter_context(tc.psum_pool(name="psum", bufs=1))
+
+        offs_sb = keep.tile([P, S // LIST_COL], U16, name="offs_sb")
+        own_sb = keep.tile([P, U // LIST_COL], U16, name="own_sb")
+        w_words = keep.tile([P, N], I32, name="w_words", align_bytes=64)
+        w_scales = keep.tile([P, N], U8, name="w_scales", align_bytes=64)
+        res_sb = keep.tile([P, U], F32, name="res_sb")
+        zero_in = keep.tile([P, 1], F32, name="zero_in")
+        zero_bias = keep.tile([P, 1], F32, name="zero_bias")
+        y_sb = keep.tile([P, S], F32, name="y_sb")
+
+        nc.vector.memset(zero_in[:], 0.0)
+        nc.scalar.activation(zero_bias[:], zero_in[:], GELU)
+        nc.vector.memset(w_scales[:].bitcast(I32), 0)
+
+        x_rows = xT.rearrange("(p j) t -> p j t", j=PACK)
+        raw = {}
+        for u in range(2):
+            t0 = 0
+            for c, width in enumerate(CHUNKS[u]):
+                raw[u, c] = keep.tile([P, 2, width], F32, name="raw_%d_%d" % (u, c))
+                nc.sync.dma_start(raw[u, c][:], x_rows[:, 2 * u : 2 * u + 2, t0 : t0 + width])
+                t0 += width
+            if u == 0:
+                nc.sync.dma_start(offs_sb[:], offs)
+        nc.sync.dma_start(w_words[:], w1_words[0].rearrange("p n t -> p (n t)").bitcast(I32))
+        for q in range(4):
+            nc.sync.dma_start(w_scales[32 * q : 32 * q + 4, :].bitcast(I32), w1_scales[0, 4 * q : 4 * q + 4, :].bitcast(I32))
+        nc.sync.dma_start(own_sb[:], own)
+        nc.sync.dma_start(res_sb[:], res)
+
+        pairs = [keep.tile([P, T], U32, name="pairs_%d" % u) for u in range(2)]
+
+        def cast(u, c, t0, a, b, engine):
+            dst = pairs[u][:, t0 + a : t0 + b].bitcast(BF16).rearrange("p (t e) -> p t e", e=2)
+            src = raw[u, c][:, :, a:b].rearrange("p e t -> p t e")
+            if engine == "v":
+                nc.vector.tensor_copy(dst, src)
+            else:
+                nc.scalar.copy(dst, src)
+
+        n_pieces = S // PIECE
+        flat = [keep.tile([P, 2, PIECE], U32, name="flat_%d" % i) for i in range(n_pieces - 1)]
+        woven = [keep.tile([P, PIECE, 2], U32, name="woven_%d" % i, align_bytes=64) for i in range(n_pieces)]
+
+        def gather(u, i):
+            window = pairs[u][:].indirect(offs_sb[:, i * PIECE // LIST_COL : (i + 1) * PIECE // LIST_COL])
+            if i < n_pieces - 1:
+                nc.vector.tensor_copy(flat[i][:, u, :], window)
+            else:
+                nc.vector.tensor_copy(woven[i][:, :, u], window)
+
+        def weave(i):
+            nc.scalar.copy(woven[i][:], flat[i][:].rearrange("p u n -> p n u"))
+
+        def multiply(i):
+            codes = keep.tile([P, PIECE], U32, name="codes_%d" % i, align_bytes=64)
+            scales = keep.tile([P, PIECE], U8, name="scales_%d" % i, align_bytes=64)
+            nc.vector.quantize_mx(out=codes[:].bitcast(FP8X4), scales=scales[:],
+                                  in_=woven[i][:].rearrange("p n u -> p (n u)").bitcast(BF16))
+            acc = psum.tile([P, PIECE], F32, name="acc_%d" % i)
+            nc.tensor.matmul_mx(out=acc[:], lhsT=w_words[:].bitcast(FP8X4), lhsT_scale=w_scales[:],
+                                rhs=codes[:].bitcast(FP8X4), rhs_scale=scales[:], start=True, stop=True)
+            nc.scalar.activation(y_sb[:, i * PIECE : (i + 1) * PIECE], acc[:], GELU, bias=zero_bias[:])
+
+        cast(0, 0, 0, 0, 1024, "v")
+        cast(0, 1, 1024, 0, 640, "v")
+        cast(0, 1, 1024, 640, 1024, "s")
+        for i in range(n_pieces):
+            gather(0, i)
+        cast(1, 0, 0, 0, 1024, "s")
+        cast(1, 1, 1024, 0, 512, "v")
+        cast(1, 2, 1536, 0, 256, "v")
+        cast(1, 3, 1792, 0, 160, "v")
+        cast(1, 3, 1792, 160, 256, "s")
+        gather(1, 0)
+        weave(0)
+        gather(1, 1)
+        weave(1)
+        gather(1, 2)
+        weave(2)
+        multiply(0)
+        multiply(1)
+        gather(1, 3)
+        multiply(2)
+        multiply(3)
+
+        r0 = 0
+        for i, width in enumerate(OUT_PIECES):
+            o = keep.tile([P, width], F32, name="o_%d" % i)
+            window = y_sb[:].indirect(own_sb[:, r0 // LIST_COL : (r0 + width) // LIST_COL])
+            nc.vector.tensor_tensor(o[:], window, res_sb[:, r0 : r0 + width], ADD)
+            nc.sync.dma_start(out[:, r0 : r0 + width], o[:])
+            r0 += width

@@ -20,8 +20,9 @@ P = 128
 PACK = 4
 LIST_COL = 16
 
-CHUNKS = ((1024, 1024), (1024, 512, 256, 256))
-PIECE = 256
+GROUPS = (("v", 384), ("s", 384), ("s", 256))
+CHUNKS = ((1024, 1024), (1024, 1024), (1024, 1024), (1024, 768, 256))
+SCALAR_CAST = 0
 OUT_PIECES = (512, 512, 512, 256, 128, 128)
 
 
@@ -45,76 +46,54 @@ def tile_picked_unmerge_gelu_e_kernel(tc, xT, w1_words, w1_scales, res, offs, ow
         nc.vector.memset(w_scales[:].bitcast(I32), 0)
 
         x_rows = xT.rearrange("(p j) t -> p j t", j=PACK)
-        raw = {}
-        for u in range(2):
+        plane32 = [keep.tile([P, T], F32, name="plane32_%d" % j) for j in range(PACK)]
+        plane16 = [keep.tile([P, T], BF16, name="plane16_%d" % j) for j in range(PACK)]
+        for j in range(PACK):
             t0 = 0
-            for c, width in enumerate(CHUNKS[u]):
-                raw[u, c] = keep.tile([P, 2, width], F32, name="raw_%d_%d" % (u, c))
-                nc.sync.dma_start(raw[u, c][:], x_rows[:, 2 * u : 2 * u + 2, t0 : t0 + width])
+            for width in CHUNKS[j]:
+                nc.sync.dma_start(plane32[j][:, t0 : t0 + width], x_rows[:, j, t0 : t0 + width])
+                if j == 0 and t0 == 0:
+                    nc.sync.dma_start(offs_sb[:], offs)
                 t0 += width
-            if u == 0:
-                nc.sync.dma_start(offs_sb[:], offs)
         nc.sync.dma_start(w_words[:], w1_words[0].rearrange("p n t -> p (n t)").bitcast(I32))
         for q in range(4):
             nc.sync.dma_start(w_scales[32 * q : 32 * q + 4, :].bitcast(I32), w1_scales[0, 4 * q : 4 * q + 4, :].bitcast(I32))
         nc.sync.dma_start(own_sb[:], own)
         nc.sync.dma_start(res_sb[:], res)
 
-        pairs = [keep.tile([P, T], U32, name="pairs_%d" % u) for u in range(2)]
+        woven = [keep.tile([P, n, PACK], BF16, name="woven_%d" % g, align_bytes=64) for g, (engine, n) in enumerate(GROUPS)]
 
-        def cast(u, c, t0, a, b, engine):
-            dst = pairs[u][:, t0 + a : t0 + b].bitcast(BF16).rearrange("p (t e) -> p t e", e=2)
-            src = raw[u, c][:, :, a:b].rearrange("p e t -> p t e")
-            if engine == "v":
-                nc.vector.tensor_copy(dst, src)
-            else:
-                nc.scalar.copy(dst, src)
+        for j in range(PACK):
+            t0 = 0
+            for width in CHUNKS[j]:
+                t1 = min(t0 + width, T - SCALAR_CAST)
+                if t1 > t0:
+                    nc.vector.tensor_copy(plane16[j][:, t0:t1], plane32[j][:, t0:t1])
+                t0 += width
+            e0 = 0
+            for g, (engine, n) in enumerate(GROUPS):
+                entries = offs_sb[:, e0 // LIST_COL : (e0 + n) // LIST_COL]
+                if engine == "v":
+                    nc.vector.tensor_copy(woven[g][:, :, j], plane32[j][:].indirect(entries))
+                else:
+                    nc.scalar.activation(woven[g][:, :, j], plane16[j][:].indirect(entries), COPY)
+                e0 += n
 
-        n_pieces = S // PIECE
-        flat = [keep.tile([P, 2, PIECE], U32, name="flat_%d" % i) for i in range(n_pieces - 1)]
-        woven = [keep.tile([P, PIECE, 2], U32, name="woven_%d" % i, align_bytes=64) for i in range(n_pieces)]
-
-        def gather(u, i):
-            window = pairs[u][:].indirect(offs_sb[:, i * PIECE // LIST_COL : (i + 1) * PIECE // LIST_COL])
-            if i < n_pieces - 1:
-                nc.vector.tensor_copy(flat[i][:, u, :], window)
-            else:
-                nc.vector.tensor_copy(woven[i][:, :, u], window)
-
-        def weave(i):
-            nc.scalar.copy(woven[i][:], flat[i][:].rearrange("p u n -> p n u"))
-
-        def multiply(i):
-            codes = keep.tile([P, PIECE], U32, name="codes_%d" % i, align_bytes=64)
-            scales = keep.tile([P, PIECE], U8, name="scales_%d" % i, align_bytes=64)
-            nc.vector.quantize_mx(out=codes[:].bitcast(FP8X4), scales=scales[:],
-                                  in_=woven[i][:].rearrange("p n u -> p (n u)").bitcast(BF16))
-            acc = psum.tile([P, PIECE], F32, name="acc_%d" % i)
-            nc.tensor.matmul_mx(out=acc[:], lhsT=w_words[:].bitcast(FP8X4), lhsT_scale=w_scales[:],
-                                rhs=codes[:].bitcast(FP8X4), rhs_scale=scales[:], start=True, stop=True)
-            nc.scalar.activation(y_sb[:, i * PIECE : (i + 1) * PIECE], acc[:], GELU, bias=zero_bias[:])
-
-        cast(0, 0, 0, 0, 1024, "v")
-        cast(0, 1, 1024, 0, 640, "v")
-        cast(0, 1, 1024, 640, 1024, "s")
-        for i in range(n_pieces):
-            gather(0, i)
-        cast(1, 0, 0, 0, 1024, "s")
-        cast(1, 1, 1024, 0, 512, "v")
-        cast(1, 2, 1536, 0, 256, "v")
-        cast(1, 3, 1792, 0, 160, "v")
-        cast(1, 3, 1792, 160, 256, "s")
-        gather(1, 0)
-        weave(0)
-        gather(1, 1)
-        weave(1)
-        gather(1, 2)
-        weave(2)
-        multiply(0)
-        multiply(1)
-        gather(1, 3)
-        multiply(2)
-        multiply(3)
+        e0 = 0
+        for g, (engine, n) in enumerate(GROUPS):
+            acc = psum.tile([P, n], F32, name="acc_%d" % g)
+            a = 0
+            for width in (512, 256, 128):
+                if n - a >= width:
+                    codes = keep.tile([P, width], U32, name="codes_%d_%d" % (g, a), align_bytes=64)
+                    scales = keep.tile([P, width], U8, name="scales_%d_%d" % (g, a), align_bytes=64)
+                    nc.vector.quantize_mx(out=codes[:].bitcast(FP8X4), scales=scales[:],
+                                          in_=woven[g][:, a : a + width, :].rearrange("p n j -> p (n j)"))
+                    nc.tensor.matmul_mx(out=acc[:, a : a + width], lhsT=w_words[:].bitcast(FP8X4), lhsT_scale=w_scales[:],
+                                        rhs=codes[:].bitcast(FP8X4), rhs_scale=scales[:], start=True, stop=True)
+                    a += width
+            nc.scalar.activation(y_sb[:, e0 : e0 + n], acc[:], GELU, bias=zero_bias[:])
+            e0 += n
 
         r0 = 0
         for i, width in enumerate(OUT_PIECES):

@@ -19,10 +19,15 @@ ADD = mybir.AluOpType.add
 P = 128
 PACK = 4
 LIST_COL = 16
+MULT = mybir.AluOpType.mult
 
-GROUPS = (("v", 384), ("s", 384), ("s", 256))
-CHUNKS = ((1024, 1024), (1024, 1024), (1024, 1024), (1024, 768, 256))
-SCALAR_CAST = 0
+GROUPS = (("v", (256,)), ("v", (256,)), ("s", (256,)), ("s", (128, 128)))
+CHUNKS = (
+    ((1024, "v"), (1024, "v")),
+    ((1024, "g"), (1024, "v")),
+    ((1024, "g"), (1024, "v")),
+    ((512, "g"), (512, "g"), (512, "g"), (512, "s")),
+)
 OUT_PIECES = (512, 512, 512, 256, 128, 128)
 
 
@@ -39,39 +44,44 @@ def tile_picked_unmerge_gelu_e_kernel(tc, xT, w1_words, w1_scales, res, offs, ow
         res_sb = keep.tile([P, U], F32, name="res_sb")
         zero_in = keep.tile([P, 1], F32, name="zero_in")
         zero_bias = keep.tile([P, 1], F32, name="zero_bias")
-        y_sb = keep.tile([P, S], F32, name="y_sb")
 
+        nc.vector.memset(w_scales[:].bitcast(I32), 0)
         nc.vector.memset(zero_in[:], 0.0)
         nc.scalar.activation(zero_bias[:], zero_in[:], GELU)
-        nc.vector.memset(w_scales[:].bitcast(I32), 0)
 
         x_rows = xT.rearrange("(p j) t -> p j t", j=PACK)
         plane32 = [keep.tile([P, T], F32, name="plane32_%d" % j) for j in range(PACK)]
-        plane16 = [keep.tile([P, T], BF16, name="plane16_%d" % j) for j in range(PACK)]
+        plane16 = [keep.tile([P, T], BF16, name="plane16_%d" % j, tag="plane16_%d" % j) for j in range(PACK)]
         for j in range(PACK):
             t0 = 0
-            for width in CHUNKS[j]:
+            for width, engine in CHUNKS[j]:
                 nc.sync.dma_start(plane32[j][:, t0 : t0 + width], x_rows[:, j, t0 : t0 + width])
                 if j == 0 and t0 == 0:
                     nc.sync.dma_start(offs_sb[:], offs)
+                    for q in range(4):
+                        nc.sync.dma_start(w_scales[32 * q : 32 * q + 4, :].bitcast(I32), w1_scales[0, 4 * q : 4 * q + 4, :].bitcast(I32))
                 t0 += width
         nc.sync.dma_start(w_words[:], w1_words[0].rearrange("p n t -> p (n t)").bitcast(I32))
-        for q in range(4):
-            nc.sync.dma_start(w_scales[32 * q : 32 * q + 4, :].bitcast(I32), w1_scales[0, 4 * q : 4 * q + 4, :].bitcast(I32))
         nc.sync.dma_start(own_sb[:], own)
         nc.sync.dma_start(res_sb[:], res)
 
-        woven = [keep.tile([P, n, PACK], BF16, name="woven_%d" % g, align_bytes=64) for g, (engine, n) in enumerate(GROUPS)]
+        woven = [keep.tile([P, sum(parts), PACK], BF16, name="woven_%d" % g, align_bytes=64) for g, (engine, parts) in enumerate(GROUPS)]
 
         for j in range(PACK):
             t0 = 0
-            for width in CHUNKS[j]:
-                t1 = min(t0 + width, T - SCALAR_CAST)
-                if t1 > t0:
-                    nc.vector.tensor_copy(plane16[j][:, t0:t1], plane32[j][:, t0:t1])
+            for width, engine in CHUNKS[j]:
+                dst = plane16[j][:, t0 : t0 + width]
+                src = plane32[j][:, t0 : t0 + width]
+                if engine == "v":
+                    nc.vector.tensor_copy(dst, src)
+                elif engine == "s":
+                    nc.scalar.copy(dst, src)
+                else:
+                    nc.gpsimd.tensor_scalar(dst, src, 1.0, 0.0, MULT, ADD)
                 t0 += width
             e0 = 0
-            for g, (engine, n) in enumerate(GROUPS):
+            for g, (engine, parts) in enumerate(GROUPS):
+                n = sum(parts)
                 entries = offs_sb[:, e0 // LIST_COL : (e0 + n) // LIST_COL]
                 if engine == "v":
                     nc.vector.tensor_copy(woven[g][:, :, j], plane32[j][:].indirect(entries))
@@ -79,21 +89,21 @@ def tile_picked_unmerge_gelu_e_kernel(tc, xT, w1_words, w1_scales, res, offs, ow
                     nc.scalar.activation(woven[g][:, :, j], plane16[j][:].indirect(entries), COPY)
                 e0 += n
 
+        y_sb = keep.tile([P, S], F32, name="y_sb", tag="plane16_%d" % (PACK - 1))
         e0 = 0
-        for g, (engine, n) in enumerate(GROUPS):
-            acc = psum.tile([P, n], F32, name="acc_%d" % g)
+        for g, (engine, parts) in enumerate(GROUPS):
             a = 0
-            for width in (512, 256, 128):
-                if n - a >= width:
-                    codes = keep.tile([P, width], U32, name="codes_%d_%d" % (g, a), align_bytes=64)
-                    scales = keep.tile([P, width], U8, name="scales_%d_%d" % (g, a), align_bytes=64)
-                    nc.vector.quantize_mx(out=codes[:].bitcast(FP8X4), scales=scales[:],
-                                          in_=woven[g][:, a : a + width, :].rearrange("p n j -> p (n j)"))
-                    nc.tensor.matmul_mx(out=acc[:, a : a + width], lhsT=w_words[:].bitcast(FP8X4), lhsT_scale=w_scales[:],
-                                        rhs=codes[:].bitcast(FP8X4), rhs_scale=scales[:], start=True, stop=True)
-                    a += width
-            nc.scalar.activation(y_sb[:, e0 : e0 + n], acc[:], GELU, bias=zero_bias[:])
-            e0 += n
+            for width in parts:
+                acc = psum.tile([P, width], F32, name="acc_%d_%d" % (g, a))
+                codes = keep.tile([P, width], U32, name="codes_%d_%d" % (g, a), align_bytes=64)
+                scales = keep.tile([P, width], U8, name="scales_%d_%d" % (g, a), align_bytes=64)
+                nc.vector.quantize_mx(out=codes[:].bitcast(FP8X4), scales=scales[:],
+                                      in_=woven[g][:, a : a + width, :].rearrange("p n j -> p (n j)"))
+                nc.tensor.matmul_mx(out=acc[:], lhsT=w_words[:].bitcast(FP8X4), lhsT_scale=w_scales[:],
+                                    rhs=codes[:].bitcast(FP8X4), rhs_scale=scales[:], start=True, stop=True)
+                nc.scalar.activation(y_sb[:, e0 : e0 + width], acc[:], GELU, bias=zero_bias[:])
+                a += width
+                e0 += width
 
         r0 = 0
         for i, width in enumerate(OUT_PIECES):

@@ -21,13 +21,10 @@ PACK = 4
 LIST_COL = 16
 MULT = mybir.AluOpType.mult
 
-GROUPS = (("v", (256,)), ("v", (256,)), ("s", (256,)), ("s", (128, 128)))
-CHUNKS = (
-    ((1024, "v"), (1024, "v")),
-    ((1024, "g"), (1024, "v")),
-    ((1024, "g"), (1024, "v")),
-    ((512, "g"), (512, "g"), (512, "g"), (512, "s")),
-)
+ORDER = (0, 1, 2, 3)
+FIRST_CAST = ((960, "g"), (1088, "s"))
+LAST_LOADS = (((640, "g"),), ((320, "g"), (448, "s")), ((448, "s"),), ((192, "v"),))
+GROUPS = (("v", (256,)), ("s", (256,)), ("s", (256,)), ("early", (128, 128)))
 OUT_PIECES = (512, 512, 512, 256, 128, 128)
 
 
@@ -50,53 +47,88 @@ def tile_picked_unmerge_gelu_e_kernel(tc, xT, w1_words, w1_scales, res, offs, ow
         nc.scalar.activation(zero_bias[:], zero_in[:], GELU)
 
         x_rows = xT.rearrange("(p j) t -> p j t", j=PACK)
+        last = ORDER[-1]
         plane32 = [keep.tile([P, T], F32, name="plane32_%d" % j) for j in range(PACK)]
-        plane16 = [keep.tile([P, T], BF16, name="plane16_%d" % j, tag="plane16_%d" % j) for j in range(PACK)]
-        for j in range(PACK):
-            t0 = 0
-            for width, engine in CHUNKS[j]:
-                nc.sync.dma_start(plane32[j][:, t0 : t0 + width], x_rows[:, j, t0 : t0 + width])
-                if j == 0 and t0 == 0:
-                    nc.sync.dma_start(offs_sb[:], offs)
-                    for q in range(4):
-                        nc.sync.dma_start(w_scales[32 * q : 32 * q + 4, :].bitcast(I32), w1_scales[0, 4 * q : 4 * q + 4, :].bitcast(I32))
-                t0 += width
+        plane16 = {j: keep.tile([P, T], BF16, name="plane16_%d" % j, tag="plane16_%d" % j) for j in (0, 1, 3)}
+        for j in ORDER[:-1]:
+            nc.sync.dma_start(plane32[j][:], x_rows[:, j, :])
+            if j == ORDER[0]:
+                nc.sync.dma_start(offs_sb[:], offs)
+                for q in range(4):
+                    nc.sync.dma_start(w_scales[32 * q : 32 * q + 4, :].bitcast(I32), w1_scales[0, 4 * q : 4 * q + 4, :].bitcast(I32))
+        t0 = 0
+        for shares in LAST_LOADS:
+            width = sum(w for w, engine in shares)
+            nc.sync.dma_start(plane32[last][:, t0 : t0 + width], x_rows[:, last, t0 : t0 + width])
+            t0 += width
         nc.sync.dma_start(w_words[:], w1_words[0].rearrange("p n t -> p (n t)").bitcast(I32))
         nc.sync.dma_start(own_sb[:], own)
         nc.sync.dma_start(res_sb[:], res)
 
-        woven = [keep.tile([P, sum(parts), PACK], BF16, name="woven_%d" % g, align_bytes=64) for g, (engine, parts) in enumerate(GROUPS)]
+        sizes = [sum(parts) for engine, parts in GROUPS]
+        starts = [sum(sizes[:g]) for g in range(len(GROUPS))]
+        n_early = sizes[-1]
+        n_late = S - n_early
+        pairs_late = keep.tile([P, 2, n_late, 2], BF16, name="pairs_late", align_bytes=64)
+        pairs_early = keep.tile([P, 2, n_early, 2], BF16, name="pairs_early", align_bytes=64)
+        woven = [keep.tile([P, n, PACK], BF16, name="woven_%d" % g, align_bytes=64) for g, n in enumerate(sizes)]
 
-        for j in range(PACK):
+        def entries(e0, n):
+            return offs_sb[:, e0 // LIST_COL : (e0 + n) // LIST_COL]
+
+        def weave_views(g, pairs, dtype):
+            dst = woven[g][:].rearrange("p n j -> p (n j)").bitcast(dtype).rearrange("p (c i u) -> p c u i", i=4, u=2)
+            src = pairs.rearrange("p u n e -> p u (n e)").bitcast(dtype).rearrange("p u (c i) -> p c u i", i=4)
+            return dst, src
+
+        def weave_late(g):
+            nc.vector.tensor_copy(*weave_views(g, pairs_late[:, :, starts[g] : starts[g] + sizes[g], :], I32))
+
+        def cast(j, shares):
             t0 = 0
-            for width, engine in CHUNKS[j]:
+            for width, engine in shares:
                 dst = plane16[j][:, t0 : t0 + width]
                 src = plane32[j][:, t0 : t0 + width]
-                if engine == "v":
-                    nc.vector.tensor_copy(dst, src)
-                elif engine == "s":
+                if engine == "s":
                     nc.scalar.copy(dst, src)
+                elif engine == "v":
+                    nc.vector.tensor_copy(dst, src)
                 else:
                     nc.gpsimd.tensor_scalar(dst, src, 1.0, 0.0, MULT, ADD)
                 t0 += width
-            e0 = 0
-            for g, (engine, parts) in enumerate(GROUPS):
-                n = sum(parts)
-                entries = offs_sb[:, e0 // LIST_COL : (e0 + n) // LIST_COL]
-                if engine == "v":
-                    nc.vector.tensor_copy(woven[g][:, :, j], plane32[j][:].indirect(entries))
-                else:
-                    nc.scalar.activation(woven[g][:, :, j], plane16[j][:].indirect(entries), COPY)
-                e0 += n
 
-        y_sb = keep.tile([P, S], F32, name="y_sb", tag="plane16_%d" % (PACK - 1))
-        e0 = 0
+        nc.vector.memset(pairs_early[:, 1].rearrange("p n e -> p (n e)").bitcast(I32), 0)
+
+        for j in (0, 1):
+            cast(j, FIRST_CAST)
+            nc.vector.tensor_copy(pairs_late[:, 0, :, j], plane32[j][:].indirect(entries(0, n_late)))
+            nc.scalar.activation(pairs_early[:, 0, :, j], plane16[j][:].indirect(entries(n_late, n_early)), COPY)
+        nc.vector.tensor_copy(pairs_early[:, 1, :, 0], plane32[2][:].indirect(entries(n_late, n_early)))
+        nc.vector.tensor_copy(pairs_late[:, 1, :, 0], plane32[2][:].indirect(entries(0, n_late)))
+        nc.scalar.copy(*weave_views(len(GROUPS) - 1, pairs_early[:], U32))
+
+        cast(last, [share for shares in LAST_LOADS for share in shares])
+
         for g, (engine, parts) in enumerate(GROUPS):
+            e0, n = starts[g], sizes[g]
+            if engine == "v":
+                nc.vector.tensor_copy(pairs_late[:, 1, e0 : e0 + n, 1], plane32[last][:].indirect(entries(e0, n)))
+            elif engine == "s":
+                nc.scalar.activation(pairs_late[:, 1, e0 : e0 + n, 1], plane16[last][:].indirect(entries(e0, n)), COPY)
+            else:
+                nc.scalar.activation(woven[g][:, :, last], plane16[last][:].indirect(entries(e0, n)), COPY)
+
+        y_sb = keep.tile([P, S], F32, name="y_sb", tag="plane16_3")
+        e0 = 0
+        weave_late(0)
+        for g, (engine, parts) in enumerate(GROUPS):
+            if g + 1 < len(GROUPS) - 1:
+                weave_late(g + 1)
             a = 0
             for width in parts:
-                acc = psum.tile([P, width], F32, name="acc_%d_%d" % (g, a))
-                codes = keep.tile([P, width], U32, name="codes_%d_%d" % (g, a), align_bytes=64)
-                scales = keep.tile([P, width], U8, name="scales_%d_%d" % (g, a), align_bytes=64)
+                acc = psum.tile([P, width], F32, name="acc_%d" % e0)
+                codes = keep.tile([P, width], U32, name="codes_%d" % e0, align_bytes=64)
+                scales = keep.tile([P, width], U8, name="scales_%d" % e0, align_bytes=64)
                 nc.vector.quantize_mx(out=codes[:].bitcast(FP8X4), scales=scales[:],
                                       in_=woven[g][:, a : a + width, :].rearrange("p n j -> p (n j)"))
                 nc.tensor.matmul_mx(out=acc[:], lhsT=w_words[:].bitcast(FP8X4), lhsT_scale=w_scales[:],

@@ -21,9 +21,9 @@ PACK = 4
 LIST_COL = 16
 MULT = mybir.AluOpType.mult
 
-ORDER = (0, 1, 2, 3)
-FIRST_CAST = ((960, "g"), (1088, "s"))
-LAST_LOADS = (((640, "g"),), ((320, "g"), (448, "s")), ((448, "s"),), ((192, "v"),))
+ORDER = (0, 2, 1, 3)
+FIRST_CAST = ((896, "g"), (1152, "s"))
+LAST_LOADS = (((640, "g"),), ((512, "g"), (256, "s")), ((384, "s"),), ((256, "s"),))
 GROUPS = (("v", (256,)), ("s", (256,)), ("s", (256,)), ("early", (128, 128)))
 OUT_PIECES = (512, 512, 512, 256, 128, 128)
 
@@ -38,7 +38,6 @@ def tile_picked_unmerge_gelu_e_kernel(tc, xT, w1_words, w1_scales, res, offs, ow
         own_sb = keep.tile([P, U // LIST_COL], U16, name="own_sb")
         w_words = keep.tile([P, N], I32, name="w_words", align_bytes=64)
         w_scales = keep.tile([P, N], U8, name="w_scales", align_bytes=64)
-        res_sb = keep.tile([P, U], F32, name="res_sb")
         zero_in = keep.tile([P, 1], F32, name="zero_in")
         zero_bias = keep.tile([P, 1], F32, name="zero_bias")
 
@@ -48,8 +47,8 @@ def tile_picked_unmerge_gelu_e_kernel(tc, xT, w1_words, w1_scales, res, offs, ow
 
         x_rows = xT.rearrange("(p j) t -> p j t", j=PACK)
         last = ORDER[-1]
-        plane32 = [keep.tile([P, T], F32, name="plane32_%d" % j) for j in range(PACK)]
-        plane16 = {j: keep.tile([P, T], BF16, name="plane16_%d" % j, tag="plane16_%d" % j) for j in (0, 1, 3)}
+        plane32 = [keep.tile([P, T], F32, name="plane32_%d" % j, tag="plane32_%d" % j) for j in range(PACK)]
+        plane16 = {j: keep.tile([P, T], BF16, name="plane16_%d" % j, tag="plane16_%d" % j) for j in (2, 3)}
         for j in ORDER[:-1]:
             nc.sync.dma_start(plane32[j][:], x_rows[:, j, :])
             if j == ORDER[0]:
@@ -63,7 +62,6 @@ def tile_picked_unmerge_gelu_e_kernel(tc, xT, w1_words, w1_scales, res, offs, ow
             t0 += width
         nc.sync.dma_start(w_words[:], w1_words[0].rearrange("p n t -> p (n t)").bitcast(I32))
         nc.sync.dma_start(own_sb[:], own)
-        nc.sync.dma_start(res_sb[:], res)
 
         sizes = [sum(parts) for engine, parts in GROUPS]
         starts = [sum(sizes[:g]) for g in range(len(GROUPS))]
@@ -99,13 +97,20 @@ def tile_picked_unmerge_gelu_e_kernel(tc, xT, w1_words, w1_scales, res, offs, ow
 
         nc.vector.memset(pairs_early[:, 1].rearrange("p n e -> p (n e)").bitcast(I32), 0)
 
-        for j in (0, 1):
-            cast(j, FIRST_CAST)
-            nc.vector.tensor_copy(pairs_late[:, 0, :, j], plane32[j][:].indirect(entries(0, n_late)))
-            nc.scalar.activation(pairs_early[:, 0, :, j], plane16[j][:].indirect(entries(n_late, n_early)), COPY)
+        n_own = sizes[0]
+        nc.vector.tensor_copy(pairs_late[:, 0, :, 0], plane32[0][:].indirect(entries(0, n_late)))
+        nc.vector.tensor_copy(pairs_early[:, 0, :, 0], plane32[0][:].indirect(entries(n_late, n_early)))
+        cast(2, FIRST_CAST)
+        nc.vector.tensor_copy(pairs_late[:, 1, :n_own, 0], plane32[2][:].indirect(entries(0, n_own)))
         nc.vector.tensor_copy(pairs_early[:, 1, :, 0], plane32[2][:].indirect(entries(n_late, n_early)))
-        nc.vector.tensor_copy(pairs_late[:, 1, :, 0], plane32[2][:].indirect(entries(0, n_late)))
+        nc.scalar.activation(pairs_late[:, 1, n_own:, 0], plane16[2][:].indirect(entries(n_own, n_late - n_own)), COPY)
+        nc.vector.tensor_copy(pairs_early[:, 0, :, 1], plane32[1][:].indirect(entries(n_late, n_early)))
+        nc.vector.tensor_copy(pairs_late[:, 0, :, 1], plane32[1][:].indirect(entries(0, n_late)))
         nc.scalar.copy(*weave_views(len(GROUPS) - 1, pairs_early[:], U32))
+
+        res_sb = keep.tile([P, U], F32, name="res_sb", tag="plane32_%d" % ORDER[-2])
+        for r0 in range(0, U, U // 2):
+            nc.sync.dma_start(res_sb[:, r0 : r0 + U // 2], res[:, r0 : r0 + U // 2])
 
         cast(last, [share for shares in LAST_LOADS for share in shares])
 

@@ -15,16 +15,26 @@ FP8X4 = mybir.dt.float8_e4m3fn_x4
 GELU = mybir.ActivationFunctionType.Gelu_apprx_tanh
 COPY = mybir.ActivationFunctionType.Copy
 ADD = mybir.AluOpType.add
+MULT = mybir.AluOpType.mult
 
 P = 128
 PACK = 4
 LIST_COL = 16
-MULT = mybir.AluOpType.mult
+QUADRANT = 32
+GROUP = 256
+GROUPS = S // GROUP
+N_LATE = S - GROUP
 
-ORDER = (0, 2, 1, 3)
-FIRST_CAST = ((896, "g"), (1152, "s"))
-LAST_LOADS = (((640, "g"),), ((512, "g"), (256, "s")), ((384, "s"),), ((256, "s"),))
-GROUPS = (("v", (256,)), ("s", (256,)), ("s", (256,)), ("early", (128, 128)))
+WHOLE_PLANES = (0, 2, 1)
+LAST = 3
+CAST_2 = (("gpsimd", 768), ("scalar", 1280))
+LAST_LOADS = (
+    (("gpsimd", 640),),
+    (("gpsimd", 416), ("scalar", 352)),
+    (("scalar", 384),),
+    (("scalar", 256),),
+)
+PASSES = ((GROUP,), (GROUP,), (GROUP,), (GROUP // 2, GROUP // 2))
 OUT_PIECES = (512, 512, 512, 256, 128, 128)
 
 
@@ -46,106 +56,96 @@ def tile_picked_unmerge_gelu_e_kernel(tc, xT, w1_words, w1_scales, res, offs, ow
         nc.scalar.activation(zero_bias[:], zero_in[:], GELU)
 
         x_rows = xT.rearrange("(p j) t -> p j t", j=PACK)
-        last = ORDER[-1]
         plane32 = [keep.tile([P, T], F32, name="plane32_%d" % j, tag="plane32_%d" % j) for j in range(PACK)]
-        plane16 = {j: keep.tile([P, T], BF16, name="plane16_%d" % j, tag="plane16_%d" % j) for j in (2, 3)}
-        for j in ORDER[:-1]:
+        plane16 = {j: keep.tile([P, T], BF16, name="plane16_%d" % j, tag="plane16_%d" % j) for j in (2, LAST)}
+        for j in WHOLE_PLANES:
             nc.sync.dma_start(plane32[j][:], x_rows[:, j, :])
-            if j == ORDER[0]:
+            if j == WHOLE_PLANES[0]:
                 nc.sync.dma_start(offs_sb[:], offs)
-                for q in range(4):
-                    nc.sync.dma_start(w_scales[32 * q : 32 * q + 4, :].bitcast(I32), w1_scales[0, 4 * q : 4 * q + 4, :].bitcast(I32))
+                for q in range(P // QUADRANT):
+                    nc.sync.dma_start(w_scales[QUADRANT * q : QUADRANT * q + 4, :].bitcast(I32),
+                                      w1_scales[0, 4 * q : 4 * q + 4, :].bitcast(I32))
         t0 = 0
         for shares in LAST_LOADS:
-            width = sum(w for w, engine in shares)
-            nc.sync.dma_start(plane32[last][:, t0 : t0 + width], x_rows[:, last, t0 : t0 + width])
-            t0 += width
+            columns = sum(width for engine, width in shares)
+            nc.sync.dma_start(plane32[LAST][:, t0 : t0 + columns], x_rows[:, LAST, t0 : t0 + columns])
+            t0 += columns
         nc.sync.dma_start(w_words[:], w1_words[0].rearrange("p n t -> p (n t)").bitcast(I32))
         nc.sync.dma_start(own_sb[:], own)
 
-        sizes = [sum(parts) for engine, parts in GROUPS]
-        starts = [sum(sizes[:g]) for g in range(len(GROUPS))]
-        n_early = sizes[-1]
-        n_late = S - n_early
-        pairs_late = keep.tile([P, 2, n_late, 2], BF16, name="pairs_late", align_bytes=64)
-        pairs_early = keep.tile([P, 2, n_early, 2], BF16, name="pairs_early", align_bytes=64)
-        woven = [keep.tile([P, n, PACK], BF16, name="woven_%d" % g, align_bytes=64) for g, n in enumerate(sizes)]
+        pairs_late = keep.tile([P, 2, N_LATE, 2], BF16, name="pairs_late", align_bytes=64)
+        pairs_early = keep.tile([P, 2, GROUP, 2], BF16, name="pairs_early", align_bytes=64)
+        woven = [keep.tile([P, GROUP, PACK], BF16, name="woven_%d" % g, align_bytes=64) for g in range(GROUPS)]
 
-        def entries(e0, n):
-            return offs_sb[:, e0 // LIST_COL : (e0 + n) // LIST_COL]
+        def picked(plane, first, count):
+            return plane[:].indirect(offs_sb[:, first // LIST_COL : (first + count) // LIST_COL])
 
-        def weave_views(g, pairs, dtype):
-            dst = woven[g][:].rearrange("p n j -> p (n j)").bitcast(dtype).rearrange("p (c i u) -> p c u i", i=4, u=2)
-            src = pairs.rearrange("p u n e -> p u (n e)").bitcast(dtype).rearrange("p u (c i) -> p c u i", i=4)
+        def weave_views(g, pairs, word):
+            dst = woven[g][:].rearrange("p n j -> p (n j)").bitcast(word).rearrange("p (n u) -> p n u", u=2)
+            src = pairs.rearrange("p u n e -> p u (n e)").bitcast(word).rearrange("p u n -> p n u")
             return dst, src
 
         def weave_late(g):
-            nc.vector.tensor_copy(*weave_views(g, pairs_late[:, :, starts[g] : starts[g] + sizes[g], :], I32))
+            nc.vector.tensor_copy(*weave_views(g, pairs_late[:, :, g * GROUP : (g + 1) * GROUP, :], I32))
 
         def cast(j, shares):
-            t0 = 0
-            for width, engine in shares:
-                dst = plane16[j][:, t0 : t0 + width]
-                src = plane32[j][:, t0 : t0 + width]
-                if engine == "s":
+            c0 = 0
+            for engine, width in shares:
+                dst = plane16[j][:, c0 : c0 + width]
+                src = plane32[j][:, c0 : c0 + width]
+                if engine == "scalar":
                     nc.scalar.copy(dst, src)
-                elif engine == "v":
-                    nc.vector.tensor_copy(dst, src)
                 else:
                     nc.gpsimd.tensor_scalar(dst, src, 1.0, 0.0, MULT, ADD)
-                t0 += width
+                c0 += width
 
         nc.vector.memset(pairs_early[:, 1].rearrange("p n e -> p (n e)").bitcast(I32), 0)
 
-        n_own = sizes[0]
-        nc.vector.tensor_copy(pairs_late[:, 0, :, 0], plane32[0][:].indirect(entries(0, n_late)))
-        nc.vector.tensor_copy(pairs_early[:, 0, :, 0], plane32[0][:].indirect(entries(n_late, n_early)))
-        cast(2, FIRST_CAST)
-        nc.vector.tensor_copy(pairs_late[:, 1, :n_own, 0], plane32[2][:].indirect(entries(0, n_own)))
-        nc.vector.tensor_copy(pairs_early[:, 1, :, 0], plane32[2][:].indirect(entries(n_late, n_early)))
-        nc.scalar.activation(pairs_late[:, 1, n_own:, 0], plane16[2][:].indirect(entries(n_own, n_late - n_own)), COPY)
-        nc.vector.tensor_copy(pairs_early[:, 0, :, 1], plane32[1][:].indirect(entries(n_late, n_early)))
-        nc.vector.tensor_copy(pairs_late[:, 0, :, 1], plane32[1][:].indirect(entries(0, n_late)))
-        nc.scalar.copy(*weave_views(len(GROUPS) - 1, pairs_early[:], U32))
+        nc.vector.tensor_copy(pairs_late[:, 0, :, 0], picked(plane32[0], 0, N_LATE))
+        nc.vector.tensor_copy(pairs_early[:, 0, :, 0], picked(plane32[0], N_LATE, GROUP))
 
-        res_sb = keep.tile([P, U], F32, name="res_sb", tag="plane32_%d" % ORDER[-2])
+        cast(2, CAST_2)
+        nc.vector.tensor_copy(pairs_late[:, 1, :GROUP, 0], picked(plane32[2], 0, GROUP))
+        nc.vector.tensor_copy(pairs_early[:, 1, :, 0], picked(plane32[2], N_LATE, GROUP))
+        nc.scalar.activation(pairs_late[:, 1, GROUP:, 0], picked(plane16[2], GROUP, N_LATE - GROUP), COPY)
+
+        nc.vector.tensor_copy(pairs_early[:, 0, :, 1], picked(plane32[1], N_LATE, GROUP))
+        nc.vector.tensor_copy(pairs_late[:, 0, :, 1], picked(plane32[1], 0, N_LATE))
+        nc.scalar.copy(*weave_views(GROUPS - 1, pairs_early[:], U32))
+
+        res_sb = keep.tile([P, U], F32, name="res_sb", tag="plane32_1")
         for r0 in range(0, U, U // 2):
             nc.sync.dma_start(res_sb[:, r0 : r0 + U // 2], res[:, r0 : r0 + U // 2])
 
-        cast(last, [share for shares in LAST_LOADS for share in shares])
+        cast(LAST, [share for shares in LAST_LOADS for share in shares])
+        nc.vector.tensor_copy(pairs_late[:, 1, :GROUP, 1], picked(plane32[LAST], 0, GROUP))
+        for e0 in range(GROUP, N_LATE, GROUP):
+            nc.scalar.activation(pairs_late[:, 1, e0 : e0 + GROUP, 1], picked(plane16[LAST], e0, GROUP), COPY)
+        nc.scalar.activation(woven[GROUPS - 1][:, :, LAST], picked(plane16[LAST], N_LATE, GROUP), COPY)
 
-        for g, (engine, parts) in enumerate(GROUPS):
-            e0, n = starts[g], sizes[g]
-            if engine == "v":
-                nc.vector.tensor_copy(pairs_late[:, 1, e0 : e0 + n, 1], plane32[last][:].indirect(entries(e0, n)))
-            elif engine == "s":
-                nc.scalar.activation(pairs_late[:, 1, e0 : e0 + n, 1], plane16[last][:].indirect(entries(e0, n)), COPY)
-            else:
-                nc.scalar.activation(woven[g][:, :, last], plane16[last][:].indirect(entries(e0, n)), COPY)
-
-        y_sb = keep.tile([P, S], F32, name="y_sb", tag="plane16_3")
+        y_sb = keep.tile([P, S], F32, name="y_sb", tag="plane16_%d" % LAST)
         e0 = 0
         weave_late(0)
-        for g, (engine, parts) in enumerate(GROUPS):
-            if g + 1 < len(GROUPS) - 1:
+        for g, widths in enumerate(PASSES):
+            if g + 1 < GROUPS - 1:
                 weave_late(g + 1)
-            a = 0
-            for width in parts:
+            n0 = 0
+            for width in widths:
                 acc = psum.tile([P, width], F32, name="acc_%d" % e0)
                 codes = keep.tile([P, width], U32, name="codes_%d" % e0, align_bytes=64)
                 scales = keep.tile([P, width], U8, name="scales_%d" % e0, align_bytes=64)
                 nc.vector.quantize_mx(out=codes[:].bitcast(FP8X4), scales=scales[:],
-                                      in_=woven[g][:, a : a + width, :].rearrange("p n j -> p (n j)"))
+                                      in_=woven[g][:, n0 : n0 + width, :].rearrange("p n j -> p (n j)"))
                 nc.tensor.matmul_mx(out=acc[:], lhsT=w_words[:].bitcast(FP8X4), lhsT_scale=w_scales[:],
                                     rhs=codes[:].bitcast(FP8X4), rhs_scale=scales[:], start=True, stop=True)
                 nc.scalar.activation(y_sb[:, e0 : e0 + width], acc[:], GELU, bias=zero_bias[:])
-                a += width
+                n0 += width
                 e0 += width
 
         r0 = 0
         for i, width in enumerate(OUT_PIECES):
-            o = keep.tile([P, width], F32, name="o_%d" % i)
-            window = y_sb[:].indirect(own_sb[:, r0 // LIST_COL : (r0 + width) // LIST_COL])
-            nc.vector.tensor_tensor(o[:], window, res_sb[:, r0 : r0 + width], ADD)
-            nc.sync.dma_start(out[:, r0 : r0 + width], o[:])
+            piece = keep.tile([P, width], F32, name="o_%d" % i)
+            fetched = y_sb[:].indirect(own_sb[:, r0 // LIST_COL : (r0 + width) // LIST_COL])
+            nc.vector.tensor_tensor(piece[:], fetched, res_sb[:, r0 : r0 + width], ADD)
+            nc.sync.dma_start(out[:, r0 : r0 + width], piece[:])
             r0 += width

@@ -62,15 +62,15 @@ def tile_picked_unmerge_gelu_e_kernel(tc, xT, w1_words, w1_scales, res, offs, ow
             nc.sync.dma_start(plane32[j][:], x_rows[:, j, :])
             if j == WHOLE_PLANES[0]:
                 nc.sync.dma_start(offs_sb[:], offs)
-                for q in range(P // QUADRANT):
-                    nc.sync.dma_start(w_scales[QUADRANT * q : QUADRANT * q + 4, :].bitcast(I32),
-                                      w1_scales[0, 4 * q : 4 * q + 4, :].bitcast(I32))
         t0 = 0
         for shares in LAST_LOADS:
             columns = sum(width for engine, width in shares)
             nc.sync.dma_start(plane32[LAST][:, t0 : t0 + columns], x_rows[:, LAST, t0 : t0 + columns])
             t0 += columns
         nc.sync.dma_start(w_words[:], w1_words[0].rearrange("p n t -> p (n t)").bitcast(I32))
+        for q in range(P // QUADRANT):
+            nc.sync.dma_start(w_scales[QUADRANT * q : QUADRANT * q + 4, :].bitcast(I32),
+                              w1_scales[0, 4 * q : 4 * q + 4, :].bitcast(I32))
         nc.sync.dma_start(own_sb[:], own)
 
         pairs_late = keep.tile([P, 2, N_LATE, 2], BF16, name="pairs_late", align_bytes=64)

@@ -35,7 +35,7 @@ LAST_LOADS = (
     (("scalar", 256),),
 )
 PASSES = ((GROUP,), (GROUP,), (GROUP,), (GROUP // 2, GROUP // 2))
-OUT_PIECES = (512, 512, 512, 256, 128, 128)
+OUT_PIECES = (896, 512, 320, 192, 128)
 
 
 def tile_picked_unmerge_gelu_e_kernel(tc, xT, w1_words, w1_scales, res, offs, own, out):
@@ -114,8 +114,10 @@ def tile_picked_unmerge_gelu_e_kernel(tc, xT, w1_words, w1_scales, res, offs, ow
         nc.scalar.copy(*weave_views(GROUPS - 1, pairs_early[:], U32))
 
         res_sb = keep.tile([P, U], F32, name="res_sb", tag="plane32_1")
-        for r0 in range(0, U, U // 2):
-            nc.sync.dma_start(res_sb[:, r0 : r0 + U // 2], res[:, r0 : r0 + U // 2])
+        r0 = 0
+        for width in OUT_PIECES:
+            nc.sync.dma_start(res_sb[:, r0 : r0 + width], res[:, r0 : r0 + width])
+            r0 += width
 
         cast(LAST, [share for shares in LAST_LOADS for share in shares])
         nc.vector.tensor_copy(pairs_late[:, 1, :GROUP, 1], picked(plane32[LAST], 0, GROUP))

@@ -32,7 +32,7 @@ LAST_LOADS = (
     (("gpsimd", 640),),
     (("gpsimd", 416), ("scalar", 352)),
     (("scalar", 384),),
-    (("scalar", 256),),
+    (("scalar", 96), ("vector", 160)),
 )
 PASSES = ((GROUP,), (GROUP,), (GROUP,), (GROUP // 2, GROUP // 2))
 OUT_PIECES = (896, 512, 320, 192, 128)
@@ -95,6 +95,8 @@ def tile_picked_unmerge_gelu_e_kernel(tc, xT, w1_words, w1_scales, res, offs, ow
                 src = plane32[j][:, c0 : c0 + width]
                 if engine == "scalar":
                     nc.scalar.copy(dst, src)
+                elif engine == "vector":
+                    nc.vector.tensor_copy(dst, src)
                 else:
                     nc.gpsimd.tensor_scalar(dst, src, 1.0, 0.0, MULT, ADD)
                 c0 += width

@@ -34,7 +34,7 @@ LAST_LOADS = (
     (("scalar", 384),),
     (("scalar", 96), ("vector", 160)),
 )
-PASSES = ((GROUP,), (GROUP,), (GROUP,), (GROUP // 2, GROUP // 2))
+PASSES = ((GROUP,),) + ((GROUP // 2, GROUP // 2),) * 3
 OUT_PIECES = (896, 512, 320, 192, 128)
 
 

@@ -29,13 +29,14 @@ WHOLE_PLANES = (0, 2, 1)
 LAST = 3
 CAST_2 = (("gpsimd", 768), ("scalar", 1280))
 LAST_LOADS = (
-    (("gpsimd", 640),),
-    (("gpsimd", 416), ("scalar", 352)),
-    (("scalar", 384),),
-    (("scalar", 96), ("vector", 160)),
+    (("gpsimd", 640), ("scalar", 320)),
+    (("gpsimd", 384), ("scalar", 320)),
+    (("scalar", 256),),
+    (("vector", 128),),
 )
 PASSES = ((GROUP,),) + ((GROUP // 2, GROUP // 2),) * 3
-OUT_PIECES = (896, 512, 320, 192, 128)
+OUT_PIECES = (992, 608, 320, 128)
+RES_LOADS = (496, 496, 304, 304, 320, 128)
 
 
 def tile_picked_unmerge_gelu_e_kernel(tc, xT, w1_words, w1_scales, res, offs, own, out):
@@ -117,7 +118,7 @@ def tile_picked_unmerge_gelu_e_kernel(tc, xT, w1_words, w1_scales, res, offs, ow
 
         res_sb = keep.tile([P, U], F32, name="res_sb", tag="plane32_1")
         r0 = 0
-        for width in OUT_PIECES:
+        for width in RES_LOADS:
             nc.sync.dma_start(res_sb[:, r0 : r0 + width], res[:, r0 : r0 + width])
             r0 += width
 

@@ -29,14 +29,15 @@ WHOLE_PLANES = (0, 2, 1)
 LAST = 3
 CAST_2 = (("gpsimd", 768), ("scalar", 1280))
 LAST_LOADS = (
-    (("gpsimd", 640), ("scalar", 320)),
-    (("gpsimd", 384), ("scalar", 320)),
+    (("gpsimd", 384),),
+    (("gpsimd", 448), ("scalar", 320)),
+    (("gpsimd", 224), ("scalar", 288)),
     (("scalar", 256),),
-    (("vector", 128),),
+    (("scalar", 128),),
 )
 PASSES = ((GROUP,),) + ((GROUP // 2, GROUP // 2),) * 3
-OUT_PIECES = (992, 608, 320, 128)
-RES_LOADS = (496, 496, 304, 304, 320, 128)
+OUT_PIECES = (896, 512, 320, 192, 128)
+RES_LOADS = (896, 512, 320, 320)
 
 
 def tile_picked_unmerge_gelu_e_kernel(tc, xT, w1_words, w1_scales, res, offs, own, out):

@@ -29,10 +29,10 @@ WHOLE_PLANES = (0, 2, 1)
 LAST = 3
 CAST_2 = (("gpsimd", 768), ("scalar", 1280))
 LAST_LOADS = (
-    (("gpsimd", 384),),
+    (("gpsimd", 512),),
     (("gpsimd", 448), ("scalar", 320)),
-    (("gpsimd", 224), ("scalar", 288)),
-    (("scalar", 256),),
+    (("gpsimd", 192), ("scalar", 256)),
+    (("scalar", 192),),
     (("scalar", 128),),
 )
 PASSES = ((GROUP,),) + ((GROUP // 2, GROUP // 2),) * 3
@@ -144,7 +144,7 @@ def tile_picked_unmerge_gelu_e_kernel(tc, xT, w1_words, w1_scales, res, offs, ow
                                       in_=woven[g][:, n0 : n0 + width, :].rearrange("p n j -> p (n j)"))
                 nc.tensor.matmul_mx(out=acc[:], lhsT=w_words[:].bitcast(FP8X4), lhsT_scale=w_scales[:],
                                     rhs=codes[:].bitcast(FP8X4), rhs_scale=scales[:], start=True, stop=True)
-                nc.scalar.activation(y_sb[:, e0 : e0 + width], acc[:], GELU, bias=zero_bias[:])
+                nc.scalar.activation(y_sb[:, e0 : e0 + width], acc[:], GELU, bias=zero_bias[:] if e0 == 0 else 0.0)
                 n0 += width
                 e0 += width
 

@@ -21,23 +21,15 @@ P = 128
 PACK = 4
 LIST_COL = 16
 QUADRANT = 32
+LAST = PACK - 1
+
 GROUP = 256
 GROUPS = S // GROUP
-N_LATE = S - GROUP
-
-WHOLE_PLANES = (0, 2, 1)
-LAST = 3
-CAST_2 = (("gpsimd", 768), ("scalar", 1280))
-LAST_LOADS = (
-    (("gpsimd", 512),),
-    (("gpsimd", 448), ("scalar", 320)),
-    (("gpsimd", 192), ("scalar", 256)),
-    (("scalar", 192),),
-    (("scalar", 128),),
-)
-PASSES = ((GROUP,),) + ((GROUP // 2, GROUP // 2),) * 3
-OUT_PIECES = (896, 512, 320, 192, 128)
-RES_LOADS = (896, 512, 320, 320)
+HALF = S // 2
+LAST_LOADS = (("gpsimd", 512), ("scalar", 512), ("gpsimd", 384), ("vector", 384), ("gpsimd", 256))
+PASSES = ((0, (256,)), (2, (128, 128)), (1, (128, 128)), (3, (128, 128)))
+OUT_PIECES = ((("vector", 288),), (("vector", 288),), (("scalar", 384),), (("vector", 160),), (("scalar", 384),),
+              (("vector", 96), ("scalar", 288)), (("scalar", 160),))
 
 
 def tile_picked_unmerge_gelu_e_kernel(tc, xT, w1_words, w1_scales, res, offs, own, out):
@@ -58,16 +50,14 @@ def tile_picked_unmerge_gelu_e_kernel(tc, xT, w1_words, w1_scales, res, offs, ow
         nc.scalar.activation(zero_bias[:], zero_in[:], GELU)
 
         x_rows = xT.rearrange("(p j) t -> p j t", j=PACK)
-        plane32 = [keep.tile([P, T], F32, name="plane32_%d" % j, tag="plane32_%d" % j) for j in range(PACK)]
-        plane16 = {j: keep.tile([P, T], BF16, name="plane16_%d" % j, tag="plane16_%d" % j) for j in (2, LAST)}
-        for j in WHOLE_PLANES:
-            nc.sync.dma_start(plane32[j][:], x_rows[:, j, :])
-            if j == WHOLE_PLANES[0]:
+        plane = [keep.tile([P, T], F32, name="plane_%d" % j, tag="plane_%d" % j) for j in range(PACK)]
+        for j in range(LAST):
+            nc.sync.dma_start(plane[j][:], x_rows[:, j, :])
+            if j == 0:
                 nc.sync.dma_start(offs_sb[:], offs)
         t0 = 0
-        for shares in LAST_LOADS:
-            columns = sum(width for engine, width in shares)
-            nc.sync.dma_start(plane32[LAST][:, t0 : t0 + columns], x_rows[:, LAST, t0 : t0 + columns])
+        for engine, columns in LAST_LOADS:
+            nc.sync.dma_start(plane[LAST][:, t0 : t0 + columns], x_rows[:, LAST, t0 : t0 + columns])
             t0 += columns
         nc.sync.dma_start(w_words[:], w1_words[0].rearrange("p n t -> p (n t)").bitcast(I32))
         for q in range(P // QUADRANT):
@@ -75,68 +65,65 @@ def tile_picked_unmerge_gelu_e_kernel(tc, xT, w1_words, w1_scales, res, offs, ow
                               w1_scales[0, 4 * q : 4 * q + 4, :].bitcast(I32))
         nc.sync.dma_start(own_sb[:], own)
 
-        pairs_late = keep.tile([P, 2, N_LATE, 2], BF16, name="pairs_late", align_bytes=64)
-        pairs_early = keep.tile([P, 2, GROUP, 2], BF16, name="pairs_early", align_bytes=64)
+        last16 = keep.tile([P, T], BF16, name="last16", tag="last16")
         woven = [keep.tile([P, GROUP, PACK], BF16, name="woven_%d" % g, align_bytes=64) for g in range(GROUPS)]
+        pairs = keep.tile([P, 2, HALF, 2], BF16, name="pairs", align_bytes=64)
+        rows01 = keep.tile([P, 2 * HALF], BF16, name="rows01")
+        rows23 = keep.tile([P, 2 * GROUP], BF16, name="rows23")
+        row2 = keep.tile([P, GROUP], BF16, name="row2")
 
-        def picked(plane, first, count):
-            return plane[:].indirect(offs_sb[:, first // LIST_COL : (first + count) // LIST_COL])
+        def picked(window, first, count):
+            return window[:].indirect(offs_sb[:, first // LIST_COL : (first + count) // LIST_COL])
 
-        def weave_views(g, pairs, word):
-            dst = woven[g][:].rearrange("p n j -> p (n j)").bitcast(word).rearrange("p (n u) -> p n u", u=2)
-            src = pairs.rearrange("p u n e -> p u (n e)").bitcast(word).rearrange("p u n -> p n u")
-            return dst, src
+        for j in range(2):
+            nc.vector.tensor_copy(pairs[:, 0, :, j], picked(plane[j], 0, HALF))
+            nc.scalar.activation(rows01[:, j * HALF : (j + 1) * HALF], picked(plane[j], HALF, HALF), COPY)
+        for g in (2, 3):
+            src = rows01[:].rearrange("p (j n) -> p n j", j=2)[:, (g - 2) * GROUP : (g - 1) * GROUP, :]
+            nc.vector.tensor_copy(woven[g][:, :, 0:2], src)
 
-        def weave_late(g):
-            nc.vector.tensor_copy(*weave_views(g, pairs_late[:, :, g * GROUP : (g + 1) * GROUP, :], I32))
+        nc.vector.tensor_copy(pairs[:, 1, :, 0], picked(plane[2], 0, HALF))
+        nc.scalar.activation(row2[:], picked(plane[2], 3 * GROUP, GROUP), COPY)
+        nc.scalar.activation(rows23[:, :GROUP], picked(plane[2], 2 * GROUP, GROUP), COPY)
+        nc.vector.tensor_copy(woven[3][:, :, 2], row2[:])
 
-        def cast(j, shares):
-            c0 = 0
-            for engine, width in shares:
-                dst = plane16[j][:, c0 : c0 + width]
-                src = plane32[j][:, c0 : c0 + width]
-                if engine == "scalar":
-                    nc.scalar.copy(dst, src)
-                elif engine == "vector":
-                    nc.vector.tensor_copy(dst, src)
-                else:
-                    nc.gpsimd.tensor_scalar(dst, src, 1.0, 0.0, MULT, ADD)
-                c0 += width
+        res_sb = keep.tile([P, U], F32, name="res_sb", tag="plane_2")
+        for r0 in range(0, U, U // 2):
+            nc.sync.dma_start(res_sb[:, r0 : r0 + U // 2], res[:, r0 : r0 + U // 2])
 
-        nc.vector.memset(pairs_early[:, 1].rearrange("p n e -> p (n e)").bitcast(I32), 0)
+        t0 = 0
+        for engine, columns in LAST_LOADS:
+            dst, src = last16[:, t0 : t0 + columns], plane[LAST][:, t0 : t0 + columns]
+            if engine == "scalar":
+                nc.scalar.copy(dst, src)
+            elif engine == "vector":
+                nc.vector.tensor_copy(dst, src)
+            else:
+                nc.gpsimd.tensor_scalar(dst, src, 1.0, 0.0, MULT, ADD)
+            t0 += columns
 
-        nc.vector.tensor_copy(pairs_late[:, 0, :, 0], picked(plane32[0], 0, N_LATE))
-        nc.vector.tensor_copy(pairs_early[:, 0, :, 0], picked(plane32[0], N_LATE, GROUP))
+        nc.vector.tensor_copy(pairs[:, 1, :GROUP, 1], picked(plane[LAST], 0, GROUP))
+        nc.scalar.activation(rows23[:, GROUP:], picked(plane[LAST], 2 * GROUP, GROUP), COPY)
+        nc.scalar.activation(pairs[:, 1, GROUP:, 1], picked(last16, GROUP, GROUP), COPY)
+        nc.scalar.activation(woven[3][:, :, LAST], picked(last16, 3 * GROUP, GROUP), COPY)
 
-        cast(2, CAST_2)
-        nc.vector.tensor_copy(pairs_late[:, 1, :GROUP, 0], picked(plane32[2], 0, GROUP))
-        nc.vector.tensor_copy(pairs_early[:, 1, :, 0], picked(plane32[2], N_LATE, GROUP))
-        nc.scalar.activation(pairs_late[:, 1, GROUP:, 0], picked(plane16[2], GROUP, N_LATE - GROUP), COPY)
+        y_sb = keep.tile([P, S], F32, name="y_sb", tag="last16")
 
-        nc.vector.tensor_copy(pairs_early[:, 0, :, 1], picked(plane32[1], N_LATE, GROUP))
-        nc.vector.tensor_copy(pairs_late[:, 0, :, 1], picked(plane32[1], 0, N_LATE))
-        nc.scalar.copy(*weave_views(GROUPS - 1, pairs_early[:], U32))
+        def finish(g):
+            if g < 2:
+                dst = woven[g][:].rearrange("p n j -> p (n j)").bitcast(I32).rearrange("p (n u) -> p n u", u=2)
+                src = pairs[:, :, g * GROUP : (g + 1) * GROUP, :].rearrange("p u n e -> p u (n e)").bitcast(I32)
+                nc.vector.tensor_copy(dst, src.rearrange("p u n -> p n u"))
+            elif g == 2:
+                nc.vector.tensor_copy(woven[g][:, :, 2:4], rows23[:].rearrange("p (j n) -> p n j", j=2))
 
-        res_sb = keep.tile([P, U], F32, name="res_sb", tag="plane32_1")
-        r0 = 0
-        for width in RES_LOADS:
-            nc.sync.dma_start(res_sb[:, r0 : r0 + width], res[:, r0 : r0 + width])
-            r0 += width
-
-        cast(LAST, [share for shares in LAST_LOADS for share in shares])
-        nc.vector.tensor_copy(pairs_late[:, 1, :GROUP, 1], picked(plane32[LAST], 0, GROUP))
-        for e0 in range(GROUP, N_LATE, GROUP):
-            nc.scalar.activation(pairs_late[:, 1, e0 : e0 + GROUP, 1], picked(plane16[LAST], e0, GROUP), COPY)
-        nc.scalar.activation(woven[GROUPS - 1][:, :, LAST], picked(plane16[LAST], N_LATE, GROUP), COPY)
-
-        y_sb = keep.tile([P, S], F32, name="y_sb", tag="plane16_%d" % LAST)
-        e0 = 0
-        weave_late(0)
-        for g, widths in enumerate(PASSES):
-            if g + 1 < GROUPS - 1:
-                weave_late(g + 1)
+        finish(PASSES[0][0])
+        for i, (g, widths) in enumerate(PASSES):
+            if i + 1 < GROUPS:
+                finish(PASSES[i + 1][0])
             n0 = 0
             for width in widths:
+                e0 = g * GROUP + n0
                 acc = psum.tile([P, width], F32, name="acc_%d" % e0)
                 codes = keep.tile([P, width], U32, name="codes_%d" % e0, align_bytes=64)
                 scales = keep.tile([P, width], U8, name="scales_%d" % e0, align_bytes=64)
@@ -146,12 +133,21 @@ def tile_picked_unmerge_gelu_e_kernel(tc, xT, w1_words, w1_scales, res, offs, ow
                                     rhs=codes[:].bitcast(FP8X4), rhs_scale=scales[:], start=True, stop=True)
                 nc.scalar.activation(y_sb[:, e0 : e0 + width], acc[:], GELU, bias=zero_bias[:] if e0 == 0 else 0.0)
                 n0 += width
-                e0 += width
 
         r0 = 0
-        for i, width in enumerate(OUT_PIECES):
-            piece = keep.tile([P, width], F32, name="o_%d" % i)
-            fetched = y_sb[:].indirect(own_sb[:, r0 // LIST_COL : (r0 + width) // LIST_COL])
-            nc.vector.tensor_tensor(piece[:], fetched, res_sb[:, r0 : r0 + width], ADD)
-            nc.sync.dma_start(out[:, r0 : r0 + width], piece[:])
-            r0 += width
+        for i, parts in enumerate(OUT_PIECES):
+            columns = sum(width for engine, width in parts)
+            piece = keep.tile([P, columns], F32, name="o_%d" % i)
+            c0 = 0
+            for engine, width in parts:
+                a, b = r0 + c0, r0 + c0 + width
+                fetched = y_sb[:].indirect(own_sb[:, a // LIST_COL : b // LIST_COL])
+                if engine == "vector":
+                    nc.vector.tensor_tensor(piece[:, c0 : c0 + width], fetched, res_sb[:, a:b], ADD)
+                else:
+                    got = keep.tile([P, width], F32, name="got_%d" % a)
+                    nc.scalar.activation(got[:], fetched, COPY)
+                    nc.vector.tensor_tensor(piece[:, c0 : c0 + width], got[:], res_sb[:, a:b], ADD)
+                c0 += width
+            nc.sync.dma_start(out[:, r0 : r0 + columns], piece[:])
+            r0 += columns

@@ -87,10 +87,6 @@ def tile_picked_unmerge_gelu_e_kernel(tc, xT, w1_words, w1_scales, res, offs, ow
         nc.scalar.activation(rows23[:, :GROUP], picked(plane[2], 2 * GROUP, GROUP), COPY)
         nc.vector.tensor_copy(woven[3][:, :, 2], row2[:])
 
-        res_sb = keep.tile([P, U], F32, name="res_sb", tag="plane_2")
-        for r0 in range(0, U, U // 2):
-            nc.sync.dma_start(res_sb[:, r0 : r0 + U // 2], res[:, r0 : r0 + U // 2])
-
         t0 = 0
         for engine, columns in LAST_LOADS:
             dst, src = last16[:, t0 : t0 + columns], plane[LAST][:, t0 : t0 + columns]
@@ -106,6 +102,10 @@ def tile_picked_unmerge_gelu_e_kernel(tc, xT, w1_words, w1_scales, res, offs, ow
         nc.scalar.activation(rows23[:, GROUP:], picked(plane[LAST], 2 * GROUP, GROUP), COPY)
         nc.scalar.activation(pairs[:, 1, GROUP:, 1], picked(last16, GROUP, GROUP), COPY)
         nc.scalar.activation(woven[3][:, :, LAST], picked(last16, 3 * GROUP, GROUP), COPY)
+
+        res_sb = keep.tile([P, U], F32, name="res_sb", tag="plane_3")
+        for r0 in range(0, U, U // 2):
+            nc.sync.dma_start(res_sb[:, r0 : r0 + U // 2], res[:, r0 : r0 + U // 2])
 
         y_sb = keep.tile([P, S], F32, name="y_sb", tag="last16")
 

@@ -26,7 +26,7 @@ LAST = PACK - 1
 GROUP = 256
 GROUPS = S // GROUP
 HALF = S // 2
-LAST_LOADS = (("gpsimd", 512), ("scalar", 512), ("gpsimd", 384), ("vector", 384), ("gpsimd", 256))
+LAST_LOADS = (("gpsimd", 704), ("scalar", 448), ("scalar", 416), ("gpsimd", 256), ("gpsimd", 224))
 PASSES = ((0, (256,)), (2, (128, 128)), (1, (128, 128)), (3, (128, 128)))
 OUT_PIECES = ((("vector", 288),), (("vector", 288),), (("scalar", 384),), (("vector", 160),), (("scalar", 384),),
               (("vector", 96), ("scalar", 288)), (("scalar", 160),))
@@ -67,25 +67,25 @@ def tile_picked_unmerge_gelu_e_kernel(tc, xT, w1_words, w1_scales, res, offs, ow
 
         last16 = keep.tile([P, T], BF16, name="last16", tag="last16")
         woven = [keep.tile([P, GROUP, PACK], BF16, name="woven_%d" % g, align_bytes=64) for g in range(GROUPS)]
-        pairs = keep.tile([P, 2, HALF, 2], BF16, name="pairs", align_bytes=64)
+        pairs = keep.tile([P, 2, GROUP, 2], BF16, name="pairs", align_bytes=64)
         rows01 = keep.tile([P, 2 * HALF], BF16, name="rows01")
-        rows23 = keep.tile([P, 2 * GROUP], BF16, name="rows23")
-        row2 = keep.tile([P, GROUP], BF16, name="row2")
+        rows23 = keep.tile([P, HALF], BF16, name="rows23")
 
         def picked(window, first, count):
             return window[:].indirect(offs_sb[:, first // LIST_COL : (first + count) // LIST_COL])
 
         for j in range(2):
-            nc.vector.tensor_copy(pairs[:, 0, :, j], picked(plane[j], 0, HALF))
+            nc.vector.tensor_copy(woven[0][:, :, j], picked(plane[j], 0, GROUP))
+            nc.vector.tensor_copy(pairs[:, 0, :, j], picked(plane[j], GROUP, GROUP))
             nc.scalar.activation(rows01[:, j * HALF : (j + 1) * HALF], picked(plane[j], HALF, HALF), COPY)
         for g in (2, 3):
             src = rows01[:].rearrange("p (j n) -> p n j", j=2)[:, (g - 2) * GROUP : (g - 1) * GROUP, :]
             nc.vector.tensor_copy(woven[g][:, :, 0:2], src)
 
-        nc.vector.tensor_copy(pairs[:, 1, :, 0], picked(plane[2], 0, HALF))
-        nc.scalar.activation(row2[:], picked(plane[2], 3 * GROUP, GROUP), COPY)
-        nc.scalar.activation(rows23[:, :GROUP], picked(plane[2], 2 * GROUP, GROUP), COPY)
-        nc.vector.tensor_copy(woven[3][:, :, 2], row2[:])
+        nc.vector.tensor_copy(woven[0][:, :, 2], picked(plane[2], 0, GROUP))
+        nc.vector.tensor_copy(pairs[:, 1, :, 0], picked(plane[2], GROUP, GROUP))
+        nc.scalar.activation(rows23[:], picked(plane[2], HALF, HALF), COPY)
+        nc.vector.tensor_copy(woven[3][:, :, 2], rows23[:, GROUP:])
 
         t0 = 0
         for engine, columns in LAST_LOADS:
@@ -98,21 +98,21 @@ def tile_picked_unmerge_gelu_e_kernel(tc, xT, w1_words, w1_scales, res, offs, ow
                 nc.gpsimd.tensor_scalar(dst, src, 1.0, 0.0, MULT, ADD)
             t0 += columns
 
-        nc.vector.tensor_copy(pairs[:, 1, :GROUP, 1], picked(plane[LAST], 0, GROUP))
+        nc.vector.tensor_copy(woven[0][:, :, LAST], picked(plane[LAST], 0, GROUP))
         nc.scalar.activation(rows23[:, GROUP:], picked(plane[LAST], 2 * GROUP, GROUP), COPY)
-        nc.scalar.activation(pairs[:, 1, GROUP:, 1], picked(last16, GROUP, GROUP), COPY)
+        nc.scalar.activation(pairs[:, 1, :, 1], picked(last16, GROUP, GROUP), COPY)
         nc.scalar.activation(woven[3][:, :, LAST], picked(last16, 3 * GROUP, GROUP), COPY)
 
-        res_sb = keep.tile([P, U], F32, name="res_sb", tag="plane_3")
+        res_sb = keep.tile([P, U], F32, name="res_sb", tag="plane_2")
         for r0 in range(0, U, U // 2):
             nc.sync.dma_start(res_sb[:, r0 : r0 + U // 2], res[:, r0 : r0 + U // 2])
 
         y_sb = keep.tile([P, S], F32, name="y_sb", tag="last16")
 
         def finish(g):
-            if g < 2:
+            if g == 1:
                 dst = woven[g][:].rearrange("p n j -> p (n j)").bitcast(I32).rearrange("p (n u) -> p n u", u=2)
-                src = pairs[:, :, g * GROUP : (g + 1) * GROUP, :].rearrange("p u n e -> p u (n e)").bitcast(I32)
+                src = pairs[:].rearrange("p u n e -> p u (n e)").bitcast(I32)
                 nc.vector.tensor_copy(dst, src.rearrange("p u n -> p n u"))
             elif g == 2:
                 nc.vector.tensor_copy(woven[g][:, :, 2:4], rows23[:].rearrange("p (j n) -> p n j", j=2))

@@ -26,10 +26,14 @@ LAST = PACK - 1
 GROUP = 256
 GROUPS = S // GROUP
 HALF = S // 2
-LAST_LOADS = (("gpsimd", 704), ("scalar", 448), ("scalar", 416), ("gpsimd", 256), ("gpsimd", 224))
+LAST_LOADS = ((("gpsimd", 416), ("scalar", 544)), (("scalar", 448), ("vector", 256)), (("gpsimd", 384),))
 PASSES = ((0, (256,)), (2, (128, 128)), (1, (128, 128)), (3, (128, 128)))
-OUT_PIECES = ((("vector", 288),), (("vector", 288),), (("scalar", 384),), (("vector", 160),), (("scalar", 384),),
-              (("vector", 96), ("scalar", 288)), (("scalar", 160),))
+OUT_PIECES = ((("vector", 416),),
+              (("vector", 416),),
+              (("scalar", 416),),
+              (("scalar", 352),),
+              (("scalar", 288),),
+              (("scalar", 160),))
 
 
 def tile_picked_unmerge_gelu_e_kernel(tc, xT, w1_words, w1_scales, res, offs, own, out):
@@ -56,7 +60,8 @@ def tile_picked_unmerge_gelu_e_kernel(tc, xT, w1_words, w1_scales, res, offs, ow
             if j == 0:
                 nc.sync.dma_start(offs_sb[:], offs)
         t0 = 0
-        for engine, columns in LAST_LOADS:
+        for shares in LAST_LOADS:
+            columns = sum(width for engine, width in shares)
             nc.sync.dma_start(plane[LAST][:, t0 : t0 + columns], x_rows[:, LAST, t0 : t0 + columns])
             t0 += columns
         nc.sync.dma_start(w_words[:], w1_words[0].rearrange("p n t -> p (n t)").bitcast(I32))
@@ -88,7 +93,7 @@ def tile_picked_unmerge_gelu_e_kernel(tc, xT, w1_words, w1_scales, res, offs, ow
         nc.vector.tensor_copy(woven[3][:, :, 2], rows23[:, GROUP:])
 
         t0 = 0
-        for engine, columns in LAST_LOADS:
+        for engine, columns in [share for shares in LAST_LOADS for share in shares]:
             dst, src = last16[:, t0 : t0 + columns], plane[LAST][:, t0 : t0 + columns]
             if engine == "scalar":
                 nc.scalar.copy(dst, src)
@@ -104,8 +109,10 @@ def tile_picked_unmerge_gelu_e_kernel(tc, xT, w1_words, w1_scales, res, offs, ow
         nc.scalar.activation(woven[3][:, :, LAST], picked(last16, 3 * GROUP, GROUP), COPY)
 
         res_sb = keep.tile([P, U], F32, name="res_sb", tag="plane_2")
-        for r0 in range(0, U, U // 2):
-            nc.sync.dma_start(res_sb[:, r0 : r0 + U // 2], res[:, r0 : r0 + U // 2])
+        r0 = 0
+        for width in (832, 608, 608,):
+            nc.sync.dma_start(res_sb[:, r0 : r0 + width], res[:, r0 : r0 + width])
+            r0 += width
 
         y_sb = keep.tile([P, S], F32, name="y_sb", tag="last16")
 

@@ -27,7 +27,7 @@ GROUP = 256
 GROUPS = S // GROUP
 HALF = S // 2
 LAST_LOADS = ((("gpsimd", 416), ("scalar", 544)), (("scalar", 448), ("vector", 256)), (("gpsimd", 384),))
-PASSES = ((0, (256,)), (2, (128, 128)), (1, (128, 128)), (3, (128, 128)))
+PASSES = ((0, (256,)), (2, (128, 128)), (1, (128, 128)), (3, (128, 64, 64)))
 OUT_PIECES = ((("vector", 416),),
               (("vector", 416),),
               (("scalar", 416),),
@@ -54,7 +54,7 @@ def tile_picked_unmerge_gelu_e_kernel(tc, xT, w1_words, w1_scales, res, offs, ow
         nc.scalar.activation(zero_bias[:], zero_in[:], GELU)
 
         x_rows = xT.rearrange("(p j) t -> p j t", j=PACK)
-        plane = [keep.tile([P, T], F32, name="plane_%d" % j, tag="plane_%d" % j) for j in range(PACK)]
+        plane = [keep.tile([P, T], F32, name="plane_%d" % j, tag="plane_%d" % j, align_bytes=64) for j in range(PACK)]
         for j in range(LAST):
             nc.sync.dma_start(plane[j][:], x_rows[:, j, :])
             if j == 0:
@@ -108,7 +108,7 @@ def tile_picked_unmerge_gelu_e_kernel(tc, xT, w1_words, w1_scales, res, offs, ow
         nc.scalar.activation(pairs[:, 1, :, 1], picked(last16, GROUP, GROUP), COPY)
         nc.scalar.activation(woven[3][:, :, LAST], picked(last16, 3 * GROUP, GROUP), COPY)
 
-        res_sb = keep.tile([P, U], F32, name="res_sb", tag="plane_2")
+        res_sb = keep.tile([P, U], F32, name="res_sb", tag="plane_2", align_bytes=64)
         r0 = 0
         for width in (832, 608, 608,):
             nc.sync.dma_start(res_sb[:, r0 : r0 + width], res[:, r0 : r0 + width])
@@ -132,7 +132,8 @@ def tile_picked_unmerge_gelu_e_kernel(tc, xT, w1_words, w1_scales, res, offs, ow
             for width in widths:
                 e0 = g * GROUP + n0
                 acc = psum.tile([P, width], F32, name="acc_%d" % e0)
-                codes = keep.tile([P, width], U32, name="codes_%d" % e0, align_bytes=64)
+                codes = keep.tile([P, width], U32, name="codes_%d" % e0, align_bytes=64,
+                                  tag="plane_3" if e0 == 0 else "codes_%d" % e0)
                 scales = keep.tile([P, width], U8, name="scales_%d" % e0, align_bytes=64)
                 nc.vector.quantize_mx(out=codes[:].bitcast(FP8X4), scales=scales[:],
                                       in_=woven[g][:, n0 : n0 + width, :].rearrange("p n j -> p (n j)"))

@@ -26,13 +26,14 @@ LAST = PACK - 1
 GROUP = 256
 GROUPS = S // GROUP
 HALF = S // 2
-LAST_LOADS = ((("gpsimd", 416), ("scalar", 544)), (("scalar", 448), ("vector", 256)), (("gpsimd", 384),))
+LAST_LOADS = ((("gpsimd", 384), ("scalar", 544)), (("scalar", 384), ("vector", 352)), (("vector", 256),), (("scalar", 128),))
 PASSES = ((0, (256,)), (2, (128, 128)), (1, (128, 128)), (3, (128, 64, 64)))
-OUT_PIECES = ((("vector", 416),),
-              (("vector", 416),),
-              (("scalar", 416),),
-              (("scalar", 352),),
-              (("scalar", 288),),
+OUT_PIECES = ((("vector", 288),),
+              (("vector", 288),),
+              (("scalar", 384),),
+              (("vector", 160),),
+              (("scalar", 384),),
+              (("vector", 96), ("scalar", 288),),
               (("scalar", 160),))
 
 
@@ -73,19 +74,17 @@ def tile_picked_unmerge_gelu_e_kernel(tc, xT, w1_words, w1_scales, res, offs, ow
         last16 = keep.tile([P, T], BF16, name="last16", tag="last16")
         woven = [keep.tile([P, GROUP, PACK], BF16, name="woven_%d" % g, align_bytes=64) for g in range(GROUPS)]
         pairs = keep.tile([P, 2, GROUP, 2], BF16, name="pairs", align_bytes=64)
-        rows01 = keep.tile([P, 2 * HALF], BF16, name="rows01")
         rows23 = keep.tile([P, HALF], BF16, name="rows23")
 
         def picked(window, first, count):
             return window[:].indirect(offs_sb[:, first // LIST_COL : (first + count) // LIST_COL])
 
         for j in range(2):
-            nc.vector.tensor_copy(woven[0][:, :, j], picked(plane[j], 0, GROUP))
             nc.vector.tensor_copy(pairs[:, 0, :, j], picked(plane[j], GROUP, GROUP))
-            nc.scalar.activation(rows01[:, j * HALF : (j + 1) * HALF], picked(plane[j], HALF, HALF), COPY)
-        for g in (2, 3):
-            src = rows01[:].rearrange("p (j n) -> p n j", j=2)[:, (g - 2) * GROUP : (g - 1) * GROUP, :]
-            nc.vector.tensor_copy(woven[g][:, :, 0:2], src)
+            for g in (0, 2, 3):
+                row = keep.tile([P, GROUP], BF16, name="row_%d_%d" % (j, g))
+                nc.scalar.activation(row[:], picked(plane[j], g * GROUP, GROUP), COPY)
+                nc.vector.tensor_copy(woven[g][:, :, j], row[:])
 
         nc.vector.tensor_copy(woven[0][:, :, 2], picked(plane[2], 0, GROUP))
         nc.vector.tensor_copy(pairs[:, 1, :, 0], picked(plane[2], GROUP, GROUP))
@@ -110,7 +109,7 @@ def tile_picked_unmerge_gelu_e_kernel(tc, xT, w1_words, w1_scales, res, offs, ow
 
         res_sb = keep.tile([P, U], F32, name="res_sb", tag="plane_2", align_bytes=64)
         r0 = 0
-        for width in (832, 608, 608,):
+        for width in (576, 1024, 448):
             nc.sync.dma_start(res_sb[:, r0 : r0 + width], res[:, r0 : r0 + width])
             r0 += width
 

@@ -30,10 +30,11 @@ LAST_LOADS = ((("gpsimd", 384), ("scalar", 544)), (("scalar", 384), ("vector", 3
 PASSES = ((0, (256,)), (2, (128, 128)), (1, (128, 128)), (3, (128, 64, 64)))
 OUT_PIECES = ((("vector", 288),),
               (("vector", 288),),
-              (("scalar", 384),),
+              (("scalar", 416),),
               (("vector", 160),),
               (("scalar", 384),),
-              (("vector", 96), ("scalar", 288),),
+              (("vector", 96),),
+              (("scalar", 256),),
               (("scalar", 160),))
 
 
@@ -109,7 +110,7 @@ def tile_picked_unmerge_gelu_e_kernel(tc, xT, w1_words, w1_scales, res, offs, ow
 
         res_sb = keep.tile([P, U], F32, name="res_sb", tag="plane_2", align_bytes=64)
         r0 = 0
-        for width in (576, 1024, 448):
+        for width in (1024, 1024):
             nc.sync.dma_start(res_sb[:, r0 : r0 + width], res[:, r0 : r0 + width])
             r0 += width
 

@@ -26,7 +26,7 @@ LAST = PACK - 1
 GROUP = 256
 GROUPS = S // GROUP
 HALF = S // 2
-LAST_LOADS = ((("gpsimd", 384), ("scalar", 544)), (("scalar", 384), ("vector", 352)), (("vector", 256),), (("scalar", 128),))
+LAST_LOADS = ((("gpsimd", 704),), (("scalar", 544),), (("scalar", 320), ("vector", 224)), (("gpsimd", 256),))
 PASSES = ((0, (256,)), (2, (128, 128)), (1, (128, 128)), (3, (128, 64, 64)))
 OUT_PIECES = ((("vector", 288),),
               (("vector", 288),),
@@ -75,7 +75,7 @@ def tile_picked_unmerge_gelu_e_kernel(tc, xT, w1_words, w1_scales, res, offs, ow
         last16 = keep.tile([P, T], BF16, name="last16", tag="last16")
         woven = [keep.tile([P, GROUP, PACK], BF16, name="woven_%d" % g, align_bytes=64) for g in range(GROUPS)]
         pairs = keep.tile([P, 2, GROUP, 2], BF16, name="pairs", align_bytes=64)
-        rows23 = keep.tile([P, HALF], BF16, name="rows23")
+        rows23 = keep.tile([P, 3, GROUP], BF16, name="rows23")
 
         def picked(window, first, count):
             return window[:].indirect(offs_sb[:, first // LIST_COL : (first + count) // LIST_COL])
@@ -89,8 +89,8 @@ def tile_picked_unmerge_gelu_e_kernel(tc, xT, w1_words, w1_scales, res, offs, ow
 
         nc.vector.tensor_copy(woven[0][:, :, 2], picked(plane[2], 0, GROUP))
         nc.vector.tensor_copy(pairs[:, 1, :, 0], picked(plane[2], GROUP, GROUP))
-        nc.scalar.activation(rows23[:], picked(plane[2], HALF, HALF), COPY)
-        nc.vector.tensor_copy(woven[3][:, :, 2], rows23[:, GROUP:])
+        nc.scalar.activation(rows23[:, 0:2, :].rearrange("p j n -> p (j n)"), picked(plane[2], HALF, HALF), COPY)
+        nc.vector.tensor_copy(woven[3][:, :, 2], rows23[:, 1, :])
 
         t0 = 0
         for engine, columns in [share for shares in LAST_LOADS for share in shares]:
@@ -104,7 +104,7 @@ def tile_picked_unmerge_gelu_e_kernel(tc, xT, w1_words, w1_scales, res, offs, ow
             t0 += columns
 
         nc.vector.tensor_copy(woven[0][:, :, LAST], picked(plane[LAST], 0, GROUP))
-        nc.scalar.activation(rows23[:, GROUP:], picked(plane[LAST], 2 * GROUP, GROUP), COPY)
+        nc.scalar.activation(rows23[:, 2, :], picked(plane[LAST], 2 * GROUP, GROUP), COPY)
         nc.scalar.activation(pairs[:, 1, :, 1], picked(last16, GROUP, GROUP), COPY)
         nc.scalar.activation(woven[3][:, :, LAST], picked(last16, 3 * GROUP, GROUP), COPY)
 
@@ -122,7 +122,7 @@ def tile_picked_unmerge_gelu_e_kernel(tc, xT, w1_words, w1_scales, res, offs, ow
                 src = pairs[:].rearrange("p u n e -> p u (n e)").bitcast(I32)
                 nc.vector.tensor_copy(dst, src.rearrange("p u n -> p n u"))
             elif g == 2:
-                nc.vector.tensor_copy(woven[g][:, :, 2:4], rows23[:].rearrange("p (j n) -> p n j", j=2))
+                nc.vector.tensor_copy(woven[g][:, :, 2:4], rows23[:, 0:3:2, :].rearrange("p j n -> p n j"))
 
         finish(PASSES[0][0])
         for i, (g, widths) in enumerate(PASSES):

@@ -82,10 +82,12 @@ def tile_picked_unmerge_gelu_e_kernel(tc, xT, w1_words, w1_scales, res, offs, ow
 
         for j in range(2):
             nc.vector.tensor_copy(pairs[:, 0, :, j], picked(plane[j], GROUP, GROUP))
-            for g in (0, 2, 3):
-                row = keep.tile([P, GROUP], BF16, name="row_%d_%d" % (j, g))
-                nc.scalar.activation(row[:], picked(plane[j], g * GROUP, GROUP), COPY)
-                nc.vector.tensor_copy(woven[g][:, :, j], row[:])
+            for groups in ((2, 3), (0,)):
+                row = keep.tile([P, len(groups), GROUP], BF16, name="row_%d_%d" % (j, groups[0]))
+                nc.scalar.activation(row[:].rearrange("p g n -> p (g n)"),
+                                     picked(plane[j], groups[0] * GROUP, len(groups) * GROUP), COPY)
+                for i, g in enumerate(groups):
+                    nc.vector.tensor_copy(woven[g][:, :, j], row[:, i, :])
 
         nc.vector.tensor_copy(woven[0][:, :, 2], picked(plane[2], 0, GROUP))
         nc.vector.tensor_copy(pairs[:, 1, :, 0], picked(plane[2], GROUP, GROUP))

from contextlib import ExitStack

import concourse.mybir as mybir

K, T, S, N, U = 512, 2048, 1024, 128, 2048
FLOPS = 2 * K * N * S

F32 = mybir.dt.float32
BF16 = mybir.dt.bfloat16
I32 = mybir.dt.int32
U32 = mybir.dt.uint32
U16 = mybir.dt.uint16
U8 = mybir.dt.uint8
FP8X4 = mybir.dt.float8_e4m3fn_x4
GELU = mybir.ActivationFunctionType.Gelu_apprx_tanh
COPY = mybir.ActivationFunctionType.Copy
ADD = mybir.AluOpType.add
MULT = mybir.AluOpType.mult

P = 128
PACK = 4
LIST_COL = 16
QUADRANT = 32
LAST = PACK - 1

GROUP = 256
GROUPS = S // GROUP
HALF = S // 2
LAST_LOADS = ((("gpsimd", 704),), (("scalar", 544),), (("scalar", 320), ("vector", 224)), (("gpsimd", 256),))
PASSES = ((0, (256,)), (2, (128, 128)), (1, (128, 128)), (3, (128, 64, 64)))
OUT_PIECES = ((("vector", 288),),
              (("vector", 288),),
              (("scalar", 416),),
              (("vector", 160),),
              (("scalar", 384),),
              (("vector", 96),),
              (("scalar", 256),),
              (("scalar", 160),))


def tile_picked_unmerge_gelu_e_kernel(tc, xT, w1_words, w1_scales, res, offs, own, out):
    nc = tc.nc
    with ExitStack() as ctx:
        keep = ctx.enter_context(tc.tile_pool(name="keep", bufs=1))
        psum = ctx.enter_context(tc.psum_pool(name="psum", bufs=1))

        offs_sb = keep.tile([P, S // LIST_COL], U16, name="offs_sb")
        own_sb = keep.tile([P, U // LIST_COL], U16, name="own_sb")
        w_words = keep.tile([P, N], I32, name="w_words", align_bytes=64)
        w_scales = keep.tile([P, N], U8, name="w_scales", align_bytes=64)
        zero_in = keep.tile([P, 1], F32, name="zero_in")
        zero_bias = keep.tile([P, 1], F32, name="zero_bias")

        nc.vector.memset(w_scales[:].bitcast(I32), 0)
        nc.vector.memset(zero_in[:], 0.0)
        nc.scalar.activation(zero_bias[:], zero_in[:], GELU)

        x_rows = xT.rearrange("(p j) t -> p j t", j=PACK)
        plane = [keep.tile([P, T], F32, name="plane_%d" % j, tag="plane_%d" % j, align_bytes=64) for j in range(PACK)]
        for j in range(LAST):
            nc.sync.dma_start(plane[j][:], x_rows[:, j, :])
            if j == 0:
                nc.sync.dma_start(offs_sb[:], offs)
        t0 = 0
        for shares in LAST_LOADS:
            columns = sum(width for engine, width in shares)
            nc.sync.dma_start(plane[LAST][:, t0 : t0 + columns], x_rows[:, LAST, t0 : t0 + columns])
            t0 += columns
        nc.sync.dma_start(w_words[:], w1_words[0].rearrange("p n t -> p (n t)").bitcast(I32))
        for q in range(P // QUADRANT):
            nc.sync.dma_start(w_scales[QUADRANT * q : QUADRANT * q + 4, :].bitcast(I32),
                              w1_scales[0, 4 * q : 4 * q + 4, :].bitcast(I32))
        nc.sync.dma_start(own_sb[:], own)

        last16 = keep.tile([P, T], BF16, name="last16", tag="last16")
        woven = [keep.tile([P, GROUP, PACK], BF16, name="woven_%d" % g, align_bytes=64) for g in range(GROUPS)]
        pairs = keep.tile([P, 2, GROUP, 2], BF16, name="pairs", align_bytes=64)
        rows23 = keep.tile([P, 3, GROUP], BF16, name="rows23")

        def picked(window, first, count):
            return window[:].indirect(offs_sb[:, first // LIST_COL : (first + count) // LIST_COL])

        for j in range(2):
            nc.vector.tensor_copy(pairs[:, 0, :, j], picked(plane[j], GROUP, GROUP))
            for groups in ((2, 3), (0,)):
                row = keep.tile([P, len(groups), GROUP], BF16, name="row_%d_%d" % (j, groups[0]))
                nc.scalar.activation(row[:].rearrange("p g n -> p (g n)"),
                                     picked(plane[j], groups[0] * GROUP, len(groups) * GROUP), COPY)
                for i, g in enumerate(groups):
                    nc.vector.tensor_copy(woven[g][:, :, j], row[:, i, :])

        nc.vector.tensor_copy(woven[0][:, :, 2], picked(plane[2], 0, GROUP))
        nc.vector.tensor_copy(pairs[:, 1, :, 0], picked(plane[2], GROUP, GROUP))
        nc.scalar.activation(rows23[:, 0:2, :].rearrange("p j n -> p (j n)"), picked(plane[2], HALF, HALF), COPY)
        nc.vector.tensor_copy(woven[3][:, :, 2], rows23[:, 1, :])

        t0 = 0
        for engine, columns in [share for shares in LAST_LOADS for share in shares]:
            dst, src = last16[:, t0 : t0 + columns], plane[LAST][:, t0 : t0 + columns]
            if engine == "scalar":
                nc.scalar.copy(dst, src)
            elif engine == "vector":
                nc.vector.tensor_copy(dst, src)
            else:
                nc.gpsimd.tensor_scalar(dst, src, 1.0, 0.0, MULT, ADD)
            t0 += columns

        nc.vector.tensor_copy(woven[0][:, :, LAST], picked(plane[LAST], 0, GROUP))
        nc.scalar.activation(rows23[:, 2, :], picked(plane[LAST], 2 * GROUP, GROUP), COPY)
        nc.scalar.activation(pairs[:, 1, :, 1], picked(last16, GROUP, GROUP), COPY)
        nc.scalar.activation(woven[3][:, :, LAST], picked(last16, 3 * GROUP, GROUP), COPY)

        res_sb = keep.tile([P, U], F32, name="res_sb", tag="plane_2", align_bytes=64)
        r0 = 0
        for width in (1024, 1024):
            nc.sync.dma_start(res_sb[:, r0 : r0 + width], res[:, r0 : r0 + width])
            r0 += width

        y_sb = keep.tile([P, S], F32, name="y_sb", tag="last16")

        def finish(g):
            if g == 1:
                dst = woven[g][:].rearrange("p n j -> p (n j)").bitcast(I32).rearrange("p (n u) -> p n u", u=2)
                src = pairs[:].rearrange("p u n e -> p u (n e)").bitcast(I32)
                nc.vector.tensor_copy(dst, src.rearrange("p u n -> p n u"))
            elif g == 2:
                nc.vector.tensor_copy(woven[g][:, :, 2:4], rows23[:, 0:3:2, :].rearrange("p j n -> p n j"))

        finish(PASSES[0][0])
        for i, (g, widths) in enumerate(PASSES):
            if i + 1 < GROUPS:
                finish(PASSES[i + 1][0])
            n0 = 0
            for width in widths:
                e0 = g * GROUP + n0
                acc = psum.tile([P, width], F32, name="acc_%d" % e0)
                codes = keep.tile([P, width], U32, name="codes_%d" % e0, align_bytes=64,
                                  tag="plane_3" if e0 == 0 else "codes_%d" % e0)
                scales = keep.tile([P, width], U8, name="scales_%d" % e0, align_bytes=64)
                nc.vector.quantize_mx(out=codes[:].bitcast(FP8X4), scales=scales[:],
                                      in_=woven[g][:, n0 : n0 + width, :].rearrange("p n j -> p (n j)"))
                nc.tensor.matmul_mx(out=acc[:], lhsT=w_words[:].bitcast(FP8X4), lhsT_scale=w_scales[:],
                                    rhs=codes[:].bitcast(FP8X4), rhs_scale=scales[:], start=True, stop=True)
                nc.scalar.activation(y_sb[:, e0 : e0 + width], acc[:], GELU, bias=zero_bias[:] if e0 == 0 else 0.0)
                n0 += width

        r0 = 0
        for i, parts in enumerate(OUT_PIECES):
            columns = sum(width for engine, width in parts)
            piece = keep.tile([P, columns], F32, name="o_%d" % i)
            c0 = 0
            for engine, width in parts:
                a, b = r0 + c0, r0 + c0 + width
                fetched = y_sb[:].indirect(own_sb[:, a // LIST_COL : b // LIST_COL])
                if engine == "vector":
                    nc.vector.tensor_tensor(piece[:, c0 : c0 + width], fetched, res_sb[:, a:b], ADD)
                else:
                    got = keep.tile([P, width], F32, name="got_%d" % a)
                    nc.scalar.activation(got[:], fetched, COPY)
                    nc.vector.tensor_tensor(piece[:, c0 : c0 + width], got[:], res_sb[:, a:b], ADD)
                c0 += width
            nc.sync.dma_start(out[:, r0 : r0 + columns], piece[:])
            r0 += columns
